import numpy as np
import ml_dtypes


def mxq(x, axis, fmt="e4m3"):
    dtype, down = {"e4m3": (ml_dtypes.float8_e4m3fn, 7), "e5m2": (ml_dtypes.float8_e5m2, 14)}[fmt]
    v = np.moveaxis(np.asarray(x, np.float32).astype(ml_dtypes.bfloat16).astype(np.float64), axis, -1)
    blocks = v.reshape(v.shape[:-1] + (-1, 32))
    amax = np.abs(blocks).max(-1, keepdims=True)
    byte = np.maximum(np.where(amax > 0, np.frexp(amax)[1] - 1 + 127, 0) - down, 1)
    scale = np.exp2(byte - 127.0)
    codes = (blocks / scale).astype(np.float32).astype(dtype).astype(np.float64)
    return np.moveaxis((codes * scale).reshape(v.shape), -1, axis)


WIDE = False


def mx_kscale(k):
    if not WIDE:
        return np.ones(k)
    levels = np.array([24, -24, 12, -12, 0])
    if k % 512:
        return np.exp2(np.random.permutation(np.resize(levels, k // 32))).repeat(32)
    a = np.empty((k // 512, 16))
    for p in range(k // 512):
        a[p, :8] = np.random.permutation(np.resize(levels, 8))
        for g in range(8):
            far = levels[np.abs(levels - a[p, g]) >= 10]
            a[p, g + 8] = far[np.random.randint(len(far))]
    return np.exp2(a.ravel()).repeat(32)


def f64(x):
    return np.asarray(x).astype(np.float64)


def striped(idx):
    return np.tile(idx.reshape(-1, 16).T, (8, 1)).astype(np.uint16)


def unstriped(offs):
    return offs[:16].T.reshape(-1).astype(np.int64)


E2M1 = np.array([0.0, 0.5, 1.0, 1.5, 2.0, 3.0, 4.0, 6.0, -0.0, -0.5, -1.0, -1.5, -2.0, -3.0, -4.0, -6.0])


def pack_weight(w, fmt):
    k, n = w.shape
    w = f64(np.asarray(w, np.float32).astype(ml_dtypes.bfloat16)).reshape(k // 32, 32, n)
    amax = np.abs(w).max(1)
    if fmt == "e4m3":
        byte = np.frexp(amax)[1] - 1 + 127 - 7
    else:
        mant, ex = np.frexp(amax / 6.0)
        byte = np.where(mant > 0.5, ex, ex - 1) + 127
    byte = np.clip(np.where(amax > 0, byte, 1), 1, 254)
    scaled = (w * np.exp2(127.0 - byte)[:, None, :]).reshape(k, n).astype(np.float32)
    by_word = np.ascontiguousarray(scaled.reshape(k // 512, 128, 4, n).transpose(0, 1, 3, 2))
    if fmt == "e4m3":
        words = by_word.astype(ml_dtypes.float8_e4m3fn).view(np.uint8)
    else:
        c = by_word.astype(ml_dtypes.float4_e2m1fn).view(np.uint8) & 0xF
        words = (c[..., 0::2] | (c[..., 1::2] << 4)).reshape(k // 512, 128, 2 * n)
    return np.ascontiguousarray(words), np.ascontiguousarray(byte.astype(np.uint8).reshape(k // 512, 16, n))


def unpack_weight(words, scales, fmt):
    g, _, n = scales.shape
    words = np.ascontiguousarray(words).reshape(g, 128, n, -1)
    if fmt == "e4m3":
        vals = words.view(ml_dtypes.float8_e4m3fn).astype(np.float64)
    else:
        nib = np.empty((g, 128, n, 4), np.uint8)
        nib[..., 0::2] = words & 0xF
        nib[..., 1::2] = words >> 4
        vals = E2M1[nib]
    vals = vals * np.repeat(np.exp2(scales.astype(np.float64) - 127.0), 8, axis=1)[..., None]
    return vals.transpose(0, 1, 3, 2).reshape(g * 512, n)


def silu(f):
    return f / (1.0 + np.exp(-np.maximum(f, -700.0)))


K, R, N, T, J = 1024, 1024, 256, 4096, 2048


def setup_inputs():
    n = np.random.standard_normal
    s = mx_kscale(K)[:, None]
    u = mx_kscale(R)[:, None]
    p_tab = pack_weight(n((K, T)) * s, "e4m3")
    p_wu = pack_weight(n((K, R)) / np.sqrt(K) / s * u.T, "e4m3")
    p_wd = pack_weight(n((R, N)) / np.sqrt(R) / u, "e4m3")
    return {
        "tab_words": p_tab[0],
        "tab_scales": p_tab[1],
        "wg": (n((K, R)) / np.sqrt(K) / s).astype(np.float32),
        "wu_words": p_wu[0],
        "wu_scales": p_wu[1],
        "wd_words": p_wd[0],
        "wd_scales": p_wd[1],
        "gT": (n((N, T))).astype(np.float32),
        "offs": striped(np.random.permutation(T)[:J]),
    }


def reference(tab_words, tab_scales, wg, wu_words, wu_scales, wd_words, wd_scales, gT, offs):
    idx = unstriped(offs)
    tab_ = unpack_weight(tab_words, tab_scales, "e4m3")[:, idx]
    wg_ = mxq(f64(wg), 0, "e4m3")
    wu_ = unpack_weight(wu_words, wu_scales, "e4m3")
    ga = wg_.T @ tab_
    ub = wu_.T @ tab_
    h = silu(ga) * ub
    h_ = mxq(h, 0, "e4m3")
    wd_ = unpack_weight(wd_words, wd_scales, "e4m3")
    y = wd_.T @ h_
    return y * f64(gT)[:, idx]

@@ -1,0 +1,316 @@
+from contextlib import ExitStack
+
+import concourse.mybir as mybir
+
+K, R, N, T, J = 1024, 1024, 256, 4096, 2048
+FLOPS = 2 * J * (2 * K * R + R * N)
+
+F32 = mybir.dt.float32
+BF16 = mybir.dt.bfloat16
+I32 = mybir.dt.int32
+U32 = mybir.dt.uint32
+U16 = mybir.dt.uint16
+U8 = mybir.dt.uint8
+FP8X4 = mybir.dt.float8_e4m3fn_x4
+MULT = mybir.AluOpType.mult
+SILU = mybir.ActivationFunctionType.Silu
+
+P = 128
+PACK = 4
+PASS = P * PACK
+CHUNK = 512
+CHUNKS = J // CHUNK
+QUARTER = CHUNK // PACK
+LIST_COLS = CHUNK // 16
+
+
+def tile_list_gmlpt_silu_gate_kernel(
+    tc, tab_words, tab_scales, wg, wu_words, wu_scales, wd_words, wd_scales, gT, offs, out
+):
+    nc = tc.nc
+    with ExitStack() as ctx:
+        lists = ctx.enter_context(tc.tile_pool(name="lists", bufs=1))
+        keep = ctx.enter_context(tc.tile_pool(name="keep", bufs=1))
+        windows = ctx.enter_context(tc.tile_pool(name="windows", bufs=2))
+        ring = ctx.enter_context(tc.tile_pool(name="ring", bufs=3))
+        psum = ctx.enter_context(tc.psum_pool(name="psum", bufs=4))
+
+        def held(shape, dtype, name):
+            return keep.tile(shape, dtype, name=name, align_bytes=64)
+
+        offsets = lists.tile([P, J // 16], U16, name="offsets")
+        tab = [windows.tile([P, T], I32, name="window", align_bytes=64) for a in range(2)]
+
+        def load_tab(a):
+            nc.sync.dma_start(out=tab[a][:], in_=tab_words[a].rearrange("p t i -> p (t i)").bitcast(I32))
+
+        def load_scales(queue, dram, width, name):
+            plane = held([P, width // 4], I32, name)
+            nc.vector.memset(plane[:], 0)
+            for quad in range(4):
+                queue.dma_start(
+                    out=plane[32 * quad : 32 * quad + 8, :],
+                    in_=dram[:, 4 * quad : 4 * quad + 4, :].bitcast(I32),
+                )
+            return plane
+
+        load_tab(0)
+        nc.sync.dma_start(offsets[:], offs)
+        tab_plane = held([P, T // 4], I32, "tab_plane")
+        for r in range(4):
+            nc.sync.dma_start(
+                out=tab_plane[r:104:4, :],
+                in_=tab_scales[:, r : r + 13, :].rearrange("a u t -> u a t").bitcast(I32),
+            )
+        nc.sync.dma_start(
+            out=tab_plane[104:, :], in_=tab_scales.rearrange("a q t -> (a q) t")[:24, :].bitcast(I32)
+        )
+        wu_plane_raw = load_scales(nc.sync, wu_scales, R, "wu_plane_raw")
+
+        warm = held([P, 16], F32, "warm")
+        warm_out = held([P, 16], F32, "warm_out")
+        nc.vector.memset(warm[:], 0.0)
+        nc.scalar.activation(out=warm_out[:], in_=warm[:], func=SILU)
+
+        wu_raw = [held([P, 2, PASS], I32, "wu_raw%d" % b) for b in range(2)]
+
+        def load_wu(b):
+            rows = wu_words.rearrange("a p r i -> p a (r i)")
+            nc.sync.dma_start(out=wu_raw[b][:], in_=rows[:, :, 4 * PASS * b : 4 * PASS * (b + 1)].bitcast(I32))
+
+        wg_raw = {}
+
+        def load_wg(b, a, parts):
+            width = PASS // parts
+            for h in range(parts):
+                raw = held([P, PACK, width], F32, "wg_raw%d%d%d" % (b, a, h))
+                c0 = PASS * b + width * h
+                nc.sync.dma_start(
+                    out=raw[:],
+                    in_=wg[PASS * a : PASS * (a + 1), c0 : c0 + width].rearrange("(p j) c -> p j c", j=PACK),
+                )
+                wg_raw[(b, a, h)] = raw
+
+        load_wu(0)
+        load_tab(1)
+        load_wg(0, 0, 2)
+        load_wg(0, 1, 2)
+        load_wu(1)
+        load_wg(1, 0, 1)
+        load_wg(1, 1, 1)
+        wd_plane = load_scales(nc.sync, wd_scales, N, "wd_plane")
+        wd = held([P, 2, N], I32, "wd")
+        nc.sync.dma_start(out=wd[:], in_=wd_words.rearrange("a p n i -> p a (n i)").bitcast(I32))
+
+        def chunk_list(c):
+            return offsets[:, LIST_COLS * c : LIST_COLS * (c + 1)]
+
+        words = {}
+        planes = {}
+
+        def gather_words(c, a):
+            words[(c, a)] = held([P, CHUNK], U32, "words%d%d" % (c, a))
+            nc.vector.tensor_copy(out=words[(c, a)][:], in_=tab[a][:].bitcast(U32).indirect(chunk_list(c)))
+
+        def gather_plane(c):
+            planes[c] = held([P, CHUNK], U8, "plane%d" % c)
+            nc.vector.tensor_copy(out=planes[c][:], in_=tab_plane[:].bitcast(U8).indirect(chunk_list(c)))
+
+        wu = {}
+
+        def permute_wu(b):
+            wu[b] = held([P, 2, PASS], I32, "wu%d" % b)
+            nc.vector.tensor_copy(
+                out=wu[b][:].rearrange("p a (t m) -> p a m t", t=PACK),
+                in_=wu_raw[b][:].rearrange("p a (m t) -> p a m t", t=PACK),
+            )
+
+        wu_plane = held([P, R], U8, "wu_plane")
+
+        def permute_wu_plane():
+            nc.vector.tensor_copy(
+                out=wu_plane[:].rearrange("p (b t m) -> p b m t", b=2, t=PACK),
+                in_=wu_plane_raw[:].bitcast(U8).rearrange("p (b m t) -> p b m t", b=2, t=PACK),
+            )
+
+        wg_bf = {}
+        wg_codes = {}
+        wg_plane = {}
+
+        def cast_wg(b, a, h, parts, on_vector):
+            if h == 0:
+                wg_bf[(b, a)] = ring.tile([P, PACK * PASS], BF16, name="wg_bf", align_bytes=64)
+            m = P // parts
+            dst = wg_bf[(b, a)][:].rearrange("p (t m j) -> p m j t", t=PACK, j=PACK)[:, m * h : m * (h + 1)]
+            src = wg_raw[(b, a, h)][:].rearrange("p j (m t) -> p m j t", t=PACK)
+            if on_vector:
+                nc.vector.tensor_copy(out=dst, in_=src)
+            else:
+                nc.scalar.copy(out=dst, in_=src)
+
+        def quantise_wg(b, a, parts):
+            wg_codes[(b, a)] = held([P, PASS], U32, "wg_codes%d%d" % (b, a))
+            wg_plane[(b, a)] = held([P, PASS], U8, "wg_plane%d%d" % (b, a))
+            w = PASS // parts
+            for s in range(parts):
+                nc.vector.quantize_mx(
+                    out=wg_codes[(b, a)][:, w * s : w * (s + 1)].bitcast(FP8X4),
+                    scales=wg_plane[(b, a)][:, w * s : w * (s + 1)],
+                    in_=wg_bf[(b, a)][:, PACK * w * s : PACK * w * (s + 1)],
+                )
+
+        h_codes = {}
+        h_plane = {}
+
+        def gate_part(c, b):
+            act = ring.tile([P, PACK, CHUNK], F32, name="act")
+            for t in range(PACK):
+                acc = psum.tile([P, CHUNK], F32, name="acc")
+                for a in range(2):
+                    nc.tensor.matmul_mx(
+                        out=acc[:],
+                        lhsT=wg_codes[(b, a)][:, P * t : P * (t + 1)].bitcast(FP8X4),
+                        lhsT_scale=wg_plane[(b, a)][:, P * t : P * (t + 1)],
+                        rhs=words[(c, a)][:].bitcast(FP8X4),
+                        rhs_scale=planes[c][4 * a :, :],
+                        start=(a == 0),
+                        stop=(a == 1),
+                    )
+                nc.scalar.activation(out=act[:, t, :], in_=acc[:], func=SILU)
+            return act
+
+        def up_quarter(c, b, q, act, h_bf):
+            cols = slice(QUARTER * q, QUARTER * (q + 1))
+            up = psum.tile([P, PACK, QUARTER], F32, name="up")
+            for t in range(PACK):
+                for a in range(2):
+                    nc.tensor.matmul_mx(
+                        out=up[:, t, :],
+                        lhsT=wu[b][:, a, P * t : P * (t + 1)].bitcast(FP8X4),
+                        lhsT_scale=wu_plane[4 * a :, PASS * b + P * t : PASS * b + P * (t + 1)],
+                        rhs=words[(c, a)][:, cols].bitcast(FP8X4),
+                        rhs_scale=planes[c][4 * a :, cols],
+                        start=(a == 0),
+                        stop=(a == 1),
+                    )
+            nc.vector.tensor_tensor(
+                out=h_bf[:, PASS * q : PASS * (q + 1)].rearrange("p (n i t) -> p n t i", i=2, t=PACK),
+                in0=up[:].rearrange("p t (n i) -> p n t i", i=2),
+                in1=act[:, :, cols].rearrange("p t (n i) -> p n t i", i=2),
+                op=MULT,
+            )
+
+        def quantise_h(c, b, h_bf, lo, hi):
+            nc.vector.quantize_mx(
+                out=h_codes[(c, b)][:, lo:hi].bitcast(FP8X4),
+                scales=h_plane[(c, b)][:, lo:hi],
+                in_=h_bf[:, PACK * lo : PACK * hi],
+            )
+
+        def down(c, nt, cols, acc):
+            for a in range(2):
+                nc.tensor.matmul_mx(
+                    out=acc,
+                    lhsT=wd[:, a, P * nt : P * (nt + 1)].bitcast(FP8X4),
+                    lhsT_scale=wd_plane[:].bitcast(U8)[4 * a :, P * nt : P * (nt + 1)],
+                    rhs=h_codes[(c, a)][:, cols].bitcast(FP8X4),
+                    rhs_scale=h_plane[(c, a)][:, cols],
+                    start=(a == 0),
+                    stop=(a == 1),
+                )
+
+        gate = []
+
+        def load_gate():
+            for nt in range(2):
+                window = windows.tile([P, T], F32, name="window", align_bytes=64)
+                nc.sync.dma_start(out=window[:], in_=gT[P * nt : P * (nt + 1), :])
+                gate.append(window)
+
+        def down_chunk(c):
+            sums = []
+            for nt in range(2):
+                acc = psum.tile([P, CHUNK], F32, name="acc")
+                down(c, nt, slice(0, CHUNK), acc[:])
+                y = ring.tile([P, CHUNK], F32, name="y")
+                nc.scalar.copy(out=y[:], in_=acc[:])
+                sums.append(y)
+            return sums
+
+        def gate_and_store(c, sums):
+            for nt in range(2):
+                res = ring.tile([P, CHUNK], F32, name="res")
+                nc.vector.tensor_tensor(
+                    out=res[:], in0=gate[nt][:].indirect(chunk_list(c)), in1=sums[nt][:], op=MULT
+                )
+                nc.sync.dma_start(out=out[P * nt : P * (nt + 1), CHUNK * c : CHUNK * (c + 1)], in_=res[:])
+
+        def unit(c, b, down_of):
+            act = gate_part(c, b)
+            sums = down_chunk(down_of) if down_of is not None else None
+            h_bf = ring.tile([P, PACK * CHUNK], BF16, name="h_bf", align_bytes=64)
+            h_codes[(c, b)] = held([P, CHUNK], U32, "h_codes%d%d" % (c, b))
+            h_plane[(c, b)] = held([P, CHUNK], U8, "h_plane%d%d" % (c, b))
+            for q in range(PACK):
+                up_quarter(c, b, q, act, h_bf)
+            quantise_h(c, b, h_bf, 0, CHUNK)
+            if down_of is not None:
+                gate_and_store(down_of, sums)
+
+        def last_unit(c, b):
+            act = gate_part(c, b)
+            h_bf = ring.tile([P, PACK * CHUNK], BF16, name="h_bf", align_bytes=64)
+            h_codes[(c, b)] = held([P, CHUNK], U32, "h_codes%d%d" % (c, b))
+            h_plane[(c, b)] = held([P, CHUNK], U8, "h_plane%d%d" % (c, b))
+            for q in range(PACK):
+                cols = slice(QUARTER * q, QUARTER * (q + 1))
+                up_quarter(c, b, q, act, h_bf)
+                quantise_h(c, b, h_bf, QUARTER * q, QUARTER * (q + 1))
+                acc = psum.tile([P, 2, QUARTER], F32, name="acc")
+                for nt in range(2):
+                    down(c, nt, cols, acc[:, nt, :])
+                y = ring.tile([P, 2, QUARTER], F32, name="y")
+                nc.scalar.copy(out=y[:], in_=acc[:])
+                res = ring.tile([P, 2, QUARTER], F32, name="res")
+                l0 = LIST_COLS * c + LIST_COLS // PACK * q
+                for nt in range(2):
+                    nc.vector.tensor_tensor(
+                        out=res[:, nt, :],
+                        in0=gate[nt][:].indirect(offsets[:, l0 : l0 + LIST_COLS // PACK]),
+                        in1=y[:, nt, :],
+                        op=MULT,
+                    )
+                c0 = CHUNK * c + QUARTER * q
+                nc.sync.dma_start(
+                    out=out[:, c0 : c0 + QUARTER].rearrange("(nt p) j -> p nt j", p=P), in_=res[:]
+                )
+
+        gather_words(0, 0)
+        gather_plane(0)
+        permute_wu(0)
+        permute_wu_plane()
+        gather_words(0, 1)
+        cast_wg(0, 0, 0, 2, False)
+        cast_wg(0, 0, 1, 2, False)
+        quantise_wg(0, 0, 1)
+        cast_wg(0, 1, 0, 2, False)
+        cast_wg(0, 1, 1, 2, False)
+        quantise_wg(0, 1, 4)
+        unit(0, 0, None)
+        for c in (1, 2):
+            gather_plane(c)
+            gather_words(c, 0)
+            gather_words(c, 1)
+            unit(c, 0, None)
+            cast_wg(1, c - 1, 0, 1, False)
+            quantise_wg(1, c - 1, 1)
+        permute_wu(1)
+        gather_plane(3)
+        gather_words(3, 0)
+        gather_words(3, 1)
+        load_gate()
+        unit(0, 1, None)
+        unit(1, 1, 0)
+        unit(2, 1, 1)
+        unit(3, 0, 2)
+        last_unit(3, 1)

@@ -31,15 +31,15 @@ def tile_list_gmlpt_silu_gate_kernel(
     with ExitStack() as ctx:
         lists = ctx.enter_context(tc.tile_pool(name="lists", bufs=1))
         keep = ctx.enter_context(tc.tile_pool(name="keep", bufs=1))
-        windows = ctx.enter_context(tc.tile_pool(name="windows", bufs=2))
         ring = ctx.enter_context(tc.tile_pool(name="ring", bufs=3))
-        psum = ctx.enter_context(tc.psum_pool(name="psum", bufs=4))
+        psum = ctx.enter_context(tc.psum_pool(name="psum", bufs=1))
+        banks = [psum.tile([P, CHUNK], F32, name="bank%d" % i) for i in range(8)]
 
         def held(shape, dtype, name):
             return keep.tile(shape, dtype, name=name, align_bytes=64)
 
         offsets = lists.tile([P, J // 16], U16, name="offsets")
-        tab = [windows.tile([P, T], I32, name="window", align_bytes=64) for a in range(2)]
+        tab = [held([P, T], I32, "tab%d" % a) for a in range(2)]
 
         def load_tab(a):
             nc.sync.dma_start(out=tab[a][:], in_=tab_words[a].rearrange("p t i -> p (t i)").bitcast(I32))
@@ -54,19 +54,6 @@ def tile_list_gmlpt_silu_gate_kernel(
                 )
             return plane
 
-        load_tab(0)
-        nc.sync.dma_start(offsets[:], offs)
-        tab_plane = held([P, T // 4], I32, "tab_plane")
-        for r in range(4):
-            nc.sync.dma_start(
-                out=tab_plane[r:104:4, :],
-                in_=tab_scales[:, r : r + 13, :].rearrange("a u t -> u a t").bitcast(I32),
-            )
-        nc.sync.dma_start(
-            out=tab_plane[104:, :], in_=tab_scales.rearrange("a q t -> (a q) t")[:24, :].bitcast(I32)
-        )
-        wu_plane_raw = load_scales(nc.sync, wu_scales, R, "wu_plane_raw")
-
         warm = held([P, 16], F32, "warm")
         warm_out = held([P, 16], F32, "warm_out")
         nc.vector.memset(warm[:], 0.0)
@@ -80,41 +67,58 @@ def tile_list_gmlpt_silu_gate_kernel(
 
         wg_raw = {}
 
-        def load_wg(b, a, parts):
-            width = PASS // parts
-            for h in range(parts):
-                raw = held([P, PACK, width], F32, "wg_raw%d%d%d" % (b, a, h))
-                c0 = PASS * b + width * h
-                nc.sync.dma_start(
-                    out=raw[:],
-                    in_=wg[PASS * a : PASS * (a + 1), c0 : c0 + width].rearrange("(p j) c -> p j c", j=PACK),
-                )
-                wg_raw[(b, a, h)] = raw
+        def load_wg(b, a):
+            raw = held([P, PACK, PASS], F32, "wg_raw%d%d" % (b, a))
+            nc.sync.dma_start(
+                out=raw[:],
+                in_=wg[PASS * a : PASS * (a + 1), PASS * b : PASS * (b + 1)].rearrange("(p j) c -> p j c", j=PACK),
+            )
+            wg_raw[(b, a)] = raw
 
-        load_wu(0)
+        gate = [held([P, T], F32, "gate%d" % nt) for nt in range(2)]
+
+        load_tab(0)
+        nc.sync.dma_start(offsets[:], offs)
+        tab_plane = held([P, T // 4], I32, "tab_plane")
+        for r in range(4):
+            nc.sync.dma_start(
+                out=tab_plane[r:104:4, :],
+                in_=tab_scales[:, r : r + 13, :].rearrange("a u t -> u a t").bitcast(I32),
+            )
+        nc.sync.dma_start(
+            out=tab_plane[104:, :], in_=tab_scales.rearrange("a q t -> (a q) t")[:24, :].bitcast(I32)
+        )
+        load_wg(0, 0)
+        wu_plane_raw = load_scales(nc.sync, wu_scales, R, "wu_plane_raw")
+        load_wg(0, 1)
         load_tab(1)
-        load_wg(0, 0, 2)
-        load_wg(0, 1, 2)
+        load_wu(0)
         load_wu(1)
-        load_wg(1, 0, 1)
-        load_wg(1, 1, 1)
+        load_wg(1, 0)
+        load_wg(1, 1)
+        for nt in range(2):
+            nc.sync.dma_start(out=gate[nt][:], in_=gT[P * nt : P * (nt + 1), :])
         wd_plane = load_scales(nc.sync, wd_scales, N, "wd_plane")
         wd = held([P, 2, N], I32, "wd")
         nc.sync.dma_start(out=wd[:], in_=wd_words.rearrange("a p n i -> p a (n i)").bitcast(I32))
 
-        def chunk_list(c):
-            return offsets[:, LIST_COLS * c : LIST_COLS * (c + 1)]
+        def chunk_list(c, count=1):
+            return offsets[:, LIST_COLS * c : LIST_COLS * (c + count)]
 
         words = {}
         planes = {}
 
-        def gather_words(c, a):
-            words[(c, a)] = held([P, CHUNK], U32, "words%d%d" % (c, a))
-            nc.vector.tensor_copy(out=words[(c, a)][:], in_=tab[a][:].bitcast(U32).indirect(chunk_list(c)))
+        def gather_words(c, a, count=1):
+            picked_words = held([P, CHUNK * count], U32, "words%d%d" % (c, a))
+            nc.vector.tensor_copy(out=picked_words[:], in_=tab[a][:].bitcast(U32).indirect(chunk_list(c, count)))
+            for i in range(count):
+                words[(c + i, a)] = picked_words[:, CHUNK * i : CHUNK * (i + 1)]
 
-        def gather_plane(c):
-            planes[c] = held([P, CHUNK], U8, "plane%d" % c)
-            nc.vector.tensor_copy(out=planes[c][:], in_=tab_plane[:].bitcast(U8).indirect(chunk_list(c)))
+        def gather_plane(c, count=1):
+            picked_plane = held([P, CHUNK * count], U8, "plane%d" % c)
+            nc.vector.tensor_copy(out=picked_plane[:], in_=tab_plane[:].bitcast(U8).indirect(chunk_list(c, count)))
+            for i in range(count):
+                planes[c + i] = picked_plane[:, CHUNK * i : CHUNK * (i + 1)]
 
         wu = {}
 
@@ -133,55 +137,50 @@ def tile_list_gmlpt_silu_gate_kernel(
                 in_=wu_plane_raw[:].bitcast(U8).rearrange("p (b m t) -> p b m t", b=2, t=PACK),
             )
 
-        wg_bf = {}
+        staging = [held([P, PACK * PASS], BF16, "staging%d" % i) for i in range(4)]
         wg_codes = {}
         wg_plane = {}
 
-        def cast_wg(b, a, h, parts, on_vector):
-            if h == 0:
-                wg_bf[(b, a)] = ring.tile([P, PACK * PASS], BF16, name="wg_bf", align_bytes=64)
+        def cast_wg(b, a, stage, h, parts):
             m = P // parts
-            dst = wg_bf[(b, a)][:].rearrange("p (t m j) -> p m j t", t=PACK, j=PACK)[:, m * h : m * (h + 1)]
-            src = wg_raw[(b, a, h)][:].rearrange("p j (m t) -> p m j t", t=PACK)
-            if on_vector:
-                nc.vector.tensor_copy(out=dst, in_=src)
-            else:
-                nc.scalar.copy(out=dst, in_=src)
+            rows = slice(m * h, m * (h + 1))
+            nc.scalar.copy(
+                out=stage[:].rearrange("p (t m j) -> p m j t", t=PACK, j=PACK)[:, rows],
+                in_=wg_raw[(b, a)][:].rearrange("p j (m t) -> p m j t", t=PACK)[:, rows],
+            )
 
-        def quantise_wg(b, a, parts):
+        def quantise_wg(b, a, stage):
             wg_codes[(b, a)] = held([P, PASS], U32, "wg_codes%d%d" % (b, a))
             wg_plane[(b, a)] = held([P, PASS], U8, "wg_plane%d%d" % (b, a))
-            w = PASS // parts
-            for s in range(parts):
-                nc.vector.quantize_mx(
-                    out=wg_codes[(b, a)][:, w * s : w * (s + 1)].bitcast(FP8X4),
-                    scales=wg_plane[(b, a)][:, w * s : w * (s + 1)],
-                    in_=wg_bf[(b, a)][:, PACK * w * s : PACK * w * (s + 1)],
-                )
+            nc.vector.quantize_mx(
+                out=wg_codes[(b, a)][:].bitcast(FP8X4), scales=wg_plane[(b, a)][:], in_=stage[:]
+            )
 
-        h_codes = {}
-        h_plane = {}
+        h_codes = {(c, b): held([P, CHUNK], U32, "h_codes%d%d" % (c, b)) for c in range(CHUNKS) for b in range(2)}
+        h_plane = {(c, b): held([P, CHUNK], U8, "h_plane%d%d" % (c, b)) for c in range(CHUNKS) for b in range(2)}
 
-        def gate_part(c, b):
+        def gate_pass(c, b, t, a, bank):
+            nc.tensor.matmul_mx(
+                out=bank[:],
+                lhsT=wg_codes[(b, a)][:, P * t : P * (t + 1)].bitcast(FP8X4),
+                lhsT_scale=wg_plane[(b, a)][:, P * t : P * (t + 1)],
+                rhs=words[(c, a)][:].bitcast(FP8X4),
+                rhs_scale=planes[c][4 * a :, :],
+                start=(a == 0),
+                stop=(a == 1),
+            )
+
+        def gate_part(c, b, first_bank, passes):
             act = ring.tile([P, PACK, CHUNK], F32, name="act")
             for t in range(PACK):
-                acc = psum.tile([P, CHUNK], F32, name="acc")
-                for a in range(2):
-                    nc.tensor.matmul_mx(
-                        out=acc[:],
-                        lhsT=wg_codes[(b, a)][:, P * t : P * (t + 1)].bitcast(FP8X4),
-                        lhsT_scale=wg_plane[(b, a)][:, P * t : P * (t + 1)],
-                        rhs=words[(c, a)][:].bitcast(FP8X4),
-                        rhs_scale=planes[c][4 * a :, :],
-                        start=(a == 0),
-                        stop=(a == 1),
-                    )
-                nc.scalar.activation(out=act[:, t, :], in_=acc[:], func=SILU)
+                for a in passes:
+                    gate_pass(c, b, t, a, banks[first_bank + t])
+                nc.scalar.activation(out=act[:, t, :], in_=banks[first_bank + t][:], func=SILU)
             return act
 
-        def up_quarter(c, b, q, act, h_bf):
+        def up_quarter(c, b, q, act, bank, stage):
             cols = slice(QUARTER * q, QUARTER * (q + 1))
-            up = psum.tile([P, PACK, QUARTER], F32, name="up")
+            up = bank[:].rearrange("p (t n) -> p t n", t=PACK)
             for t in range(PACK):
                 for a in range(2):
                     nc.tensor.matmul_mx(
@@ -194,17 +193,21 @@ def tile_list_gmlpt_silu_gate_kernel(
                         stop=(a == 1),
                     )
             nc.vector.tensor_tensor(
-                out=h_bf[:, PASS * q : PASS * (q + 1)].rearrange("p (n i t) -> p n t i", i=2, t=PACK),
-                in0=up[:].rearrange("p t (n i) -> p n t i", i=2),
+                out=stage[:, PASS * q : PASS * (q + 1)].rearrange("p (n i t) -> p n t i", i=2, t=PACK),
+                in0=up.rearrange("p t (n i) -> p n t i", i=2),
                 in1=act[:, :, cols].rearrange("p t (n i) -> p n t i", i=2),
                 op=MULT,
             )
 
-        def quantise_h(c, b, h_bf, lo, hi):
+        def up_part(c, b, act, first_bank, stage):
+            for q in range(PACK):
+                up_quarter(c, b, q, act, banks[first_bank + q], stage)
+
+        def quantise_h(c, b, stage, lo, hi):
             nc.vector.quantize_mx(
                 out=h_codes[(c, b)][:, lo:hi].bitcast(FP8X4),
                 scales=h_plane[(c, b)][:, lo:hi],
-                in_=h_bf[:, PACK * lo : PACK * hi],
+                in_=stage[:, PACK * lo : PACK * hi],
             )
 
         def down(c, nt, cols, acc):
@@ -219,98 +222,107 @@ def tile_list_gmlpt_silu_gate_kernel(
                     stop=(a == 1),
                 )
 
-        gate = []
-
-        def load_gate():
-            for nt in range(2):
-                window = windows.tile([P, T], F32, name="window", align_bytes=64)
-                nc.sync.dma_start(out=window[:], in_=gT[P * nt : P * (nt + 1), :])
-                gate.append(window)
-
         def down_chunk(c):
             sums = []
             for nt in range(2):
-                acc = psum.tile([P, CHUNK], F32, name="acc")
-                down(c, nt, slice(0, CHUNK), acc[:])
+                down(c, nt, slice(0, CHUNK), banks[nt][:])
                 y = ring.tile([P, CHUNK], F32, name="y")
-                nc.scalar.copy(out=y[:], in_=acc[:])
+                nc.scalar.copy(out=y[:], in_=banks[nt][:])
                 sums.append(y)
             return sums
 
-        def gate_and_store(c, sums):
+        def gate_and_store(c, nt, y):
+            res = ring.tile([P, CHUNK], F32, name="res")
+            nc.vector.tensor_tensor(out=res[:], in0=gate[nt][:].indirect(chunk_list(c)), in1=y[:], op=MULT)
+            nc.sync.dma_start(out=out[P * nt : P * (nt + 1), CHUNK * c : CHUNK * (c + 1)], in_=res[:])
+
+        def pick_gate(c, nt):
+            nc.vector.tensor_copy(out=picked[c][:, nt, :], in_=gate[nt][:].indirect(chunk_list(c)))
+
+        def scale_and_store(c, nt, bank):
+            res = held([P, CHUNK], F32, "res_late%d" % nt)
+            nc.vector.tensor_tensor(out=res[:], in0=bank[:], in1=picked[c][:, nt, :], op=MULT)
+            nc.sync.dma_start(out=out[P * nt : P * (nt + 1), CHUNK * c : CHUNK * (c + 1)], in_=res[:])
+
+        def quarter_view(q):
+            return banks[q][:, : 2 * QUARTER].rearrange("p (nt n) -> p nt n", nt=2)
+
+        def down_quarter(c, q):
             for nt in range(2):
-                res = ring.tile([P, CHUNK], F32, name="res")
-                nc.vector.tensor_tensor(
-                    out=res[:], in0=gate[nt][:].indirect(chunk_list(c)), in1=sums[nt][:], op=MULT
-                )
-                nc.sync.dma_start(out=out[P * nt : P * (nt + 1), CHUNK * c : CHUNK * (c + 1)], in_=res[:])
+                down(c, nt, slice(QUARTER * q, QUARTER * (q + 1)), quarter_view(q)[:, nt, :])
 
-        def unit(c, b, down_of):
-            act = gate_part(c, b)
-            sums = down_chunk(down_of) if down_of is not None else None
-            h_bf = ring.tile([P, PACK * CHUNK], BF16, name="h_bf", align_bytes=64)
-            h_codes[(c, b)] = held([P, CHUNK], U32, "h_codes%d%d" % (c, b))
-            h_plane[(c, b)] = held([P, CHUNK], U8, "h_plane%d%d" % (c, b))
-            for q in range(PACK):
-                up_quarter(c, b, q, act, h_bf)
-            quantise_h(c, b, h_bf, 0, CHUNK)
-            if down_of is not None:
-                gate_and_store(down_of, sums)
+        def scale_and_store_quarter(c, q):
+            res = held([P, 2, QUARTER], F32, "res_last%d" % q)
+            nc.vector.tensor_tensor(
+                out=res[:], in0=quarter_view(q), in1=picked[c][:, :, QUARTER * q : QUARTER * (q + 1)], op=MULT
+            )
+            c0 = CHUNK * c + QUARTER * q
+            nc.sync.dma_start(out=out[:, c0 : c0 + QUARTER].rearrange("(nt p) j -> p nt j", p=P), in_=res[:])
 
-        def last_unit(c, b):
-            act = gate_part(c, b)
-            h_bf = ring.tile([P, PACK * CHUNK], BF16, name="h_bf", align_bytes=64)
-            h_codes[(c, b)] = held([P, CHUNK], U32, "h_codes%d%d" % (c, b))
-            h_plane[(c, b)] = held([P, CHUNK], U8, "h_plane%d%d" % (c, b))
-            for q in range(PACK):
-                cols = slice(QUARTER * q, QUARTER * (q + 1))
-                up_quarter(c, b, q, act, h_bf)
-                quantise_h(c, b, h_bf, QUARTER * q, QUARTER * (q + 1))
-                acc = psum.tile([P, 2, QUARTER], F32, name="acc")
-                for nt in range(2):
-                    down(c, nt, cols, acc[:, nt, :])
-                y = ring.tile([P, 2, QUARTER], F32, name="y")
-                nc.scalar.copy(out=y[:], in_=acc[:])
-                res = ring.tile([P, 2, QUARTER], F32, name="res")
-                l0 = LIST_COLS * c + LIST_COLS // PACK * q
-                for nt in range(2):
-                    nc.vector.tensor_tensor(
-                        out=res[:, nt, :],
-                        in0=gate[nt][:].indirect(offsets[:, l0 : l0 + LIST_COLS // PACK]),
-                        in1=y[:, nt, :],
-                        op=MULT,
-                    )
-                c0 = CHUNK * c + QUARTER * q
-                nc.sync.dma_start(
-                    out=out[:, c0 : c0 + QUARTER].rearrange("(nt p) j -> p nt j", p=P), in_=res[:]
-                )
+        picked = {2: wg_raw[(1, 1)][:, 0:2, :], 3: wg_raw[(1, 1)][:, 2:4, :]}
 
-        gather_words(0, 0)
-        gather_plane(0)
-        permute_wu(0)
+        gather_words(0, 0, 2)
+        gather_plane(0, 2)
         permute_wu_plane()
+        cast_wg(0, 0, staging[0], 0, 1)
+        cast_wg(0, 1, staging[1], 0, 1)
+        gather_words(2, 0, 2)
+        quantise_wg(0, 0, staging[0])
+        for c in range(2):
+            for t in range(PACK):
+                gate_pass(c, 0, t, 0, banks[4 * c + t])
+        gather_plane(2)
+        quantise_wg(0, 1, staging[1])
         gather_words(0, 1)
-        cast_wg(0, 0, 0, 2, False)
-        cast_wg(0, 0, 1, 2, False)
-        quantise_wg(0, 0, 1)
-        cast_wg(0, 1, 0, 2, False)
-        cast_wg(0, 1, 1, 2, False)
-        quantise_wg(0, 1, 4)
-        unit(0, 0, None)
-        for c in (1, 2):
-            gather_plane(c)
-            gather_words(c, 0)
-            gather_words(c, 1)
-            unit(c, 0, None)
-            cast_wg(1, c - 1, 0, 1, False)
-            quantise_wg(1, c - 1, 1)
-        permute_wu(1)
+        act0 = gate_part(0, 0, 0, (1,))
+        gather_words(1, 1)
+        act1 = gate_part(1, 0, 4, (1,))
+        permute_wu(0)
+        gather_words(2, 1)
+        up_part(0, 0, act0, 0, staging[2])
+        quantise_h(0, 0, staging[2], 0, CHUNK)
+        up_part(1, 0, act1, 4, staging[3])
+        cast_wg(1, 0, staging[2], 0, 2)
+        act = gate_part(2, 0, 0, (0, 1))
+        cast_wg(1, 0, staging[2], 1, 2)
         gather_plane(3)
-        gather_words(3, 0)
+        quantise_h(1, 0, staging[3], 0, CHUNK)
         gather_words(3, 1)
-        load_gate()
-        unit(0, 1, None)
-        unit(1, 1, 0)
-        unit(2, 1, 1)
-        unit(3, 0, 2)
-        last_unit(3, 1)
+        up_part(2, 0, act, 4, staging[0])
+        cast_wg(1, 1, staging[3], 0, 2)
+        act = gate_part(3, 0, 0, (0, 1))
+        cast_wg(1, 1, staging[3], 1, 2)
+        quantise_wg(1, 0, staging[2])
+        quantise_h(2, 0, staging[0], 0, CHUNK)
+        permute_wu(1)
+        for q in range(PACK):
+            up_quarter(3, 0, q, act, banks[4 + q], staging[1])
+            if q == 1:
+                quantise_wg(1, 1, staging[3])
+        act = gate_part(0, 1, 0, (0, 1))
+        pick_gate(2, 0)
+        quantise_h(3, 0, staging[1], 0, CHUNK)
+        up_part(0, 1, act, 4, staging[0])
+        quantise_h(0, 1, staging[0], 0, CHUNK)
+        pick_gate(3, 0)
+        pick_gate(2, 1)
+        pick_gate(3, 1)
+        for c in (1, 2):
+            act = gate_part(c, 1, 0, (0, 1))
+            sums = down_chunk(c - 1)
+            up_part(c, 1, act, 4, staging[c])
+            quantise_h(c, 1, staging[c], 0, CHUNK)
+            gate_and_store(c - 1, 0, sums[0])
+            gate_and_store(c - 1, 1, sums[1])
+        act = gate_part(3, 1, 0, (0, 1))
+        for nt in range(2):
+            down(2, nt, slice(0, CHUNK), banks[4 + nt][:])
+            scale_and_store(2, nt, banks[4 + nt])
+        for q in range(PACK + 1):
+            if q < PACK:
+                up_quarter(3, 1, q, act, banks[4 + (q + 2) % 4], staging[3])
+            if q >= 1:
+                quantise_h(3, 1, staging[3], QUARTER * (q - 1), QUARTER * q)
+        for q in range(PACK):
+            down_quarter(3, q)
+            scale_and_store_quarter(3, q)

@@ -123,37 +123,37 @@ def tile_list_gmlpt_silu_gate_kernel(
         wu = {}
 
         def permute_wu(b):
-            wu[b] = held([P, 2, PASS], I32, "wu%d" % b)
+            wu[b] = held([P, PACK, 2, P], I32, "wu%d" % b)
             nc.vector.tensor_copy(
-                out=wu[b][:].rearrange("p a (t m) -> p a m t", t=PACK),
-                in_=wu_raw[b][:].rearrange("p a (m t) -> p a m t", t=PACK),
+                out=wu[b][:].rearrange("p t a (c i) -> p (a c) t i", i=4),
+                in_=wu_raw[b][:].rearrange("p a (c i t) -> p (a c) t i", i=4, t=PACK),
             )
 
-        wu_plane = held([P, R], U8, "wu_plane")
+        wu_plane = held([P, PACK, 2, P], U8, "wu_plane")
 
         def permute_wu_plane():
             nc.vector.tensor_copy(
-                out=wu_plane[:].rearrange("p (b t m) -> p b m t", b=2, t=PACK),
-                in_=wu_plane_raw[:].bitcast(U8).rearrange("p (b m t) -> p b m t", b=2, t=PACK),
+                out=wu_plane[:].rearrange("p t b (c i) -> p (b c) t i", i=16),
+                in_=wu_plane_raw[:].bitcast(U8).rearrange("p (c i t) -> p c t i", i=16, t=PACK),
             )
 
         staging = [held([P, PACK * PASS], BF16, "staging%d" % i) for i in range(4)]
-        wg_codes = {}
-        wg_plane = {}
+        late_stage = keep.tile([P, PACK * PASS], BF16, name="late_stage", tag="wu_raw0", align_bytes=64)
+        wg_codes = {(b, a): held([P, PASS], U32, "wg_codes%d%d" % (b, a)) for b in range(2) for a in range(2)}
+        wg_plane = {(b, a): held([P, PASS], U8, "wg_plane%d%d" % (b, a)) for b in range(2) for a in range(2)}
 
-        def cast_wg(b, a, stage, h, parts):
-            m = P // parts
-            rows = slice(m * h, m * (h + 1))
+        def cast_wg(b, a, stage, half):
+            pair = slice(2 * half, 2 * half + 2)
             nc.scalar.copy(
-                out=stage[:].rearrange("p (t m j) -> p m j t", t=PACK, j=PACK)[:, rows],
-                in_=wg_raw[(b, a)][:].rearrange("p j (m t) -> p m j t", t=PACK)[:, rows],
+                out=stage[:].rearrange("p (t m j) -> p m t j", t=PACK, j=PACK)[:, :, pair],
+                in_=wg_raw[(b, a)][:].rearrange("p j (m t) -> p m t j", t=PACK)[:, :, pair],
             )
 
-        def quantise_wg(b, a, stage):
-            wg_codes[(b, a)] = held([P, PASS], U32, "wg_codes%d%d" % (b, a))
-            wg_plane[(b, a)] = held([P, PASS], U8, "wg_plane%d%d" % (b, a))
+        def quantise_wg(b, a, stage, lo, hi):
             nc.vector.quantize_mx(
-                out=wg_codes[(b, a)][:].bitcast(FP8X4), scales=wg_plane[(b, a)][:], in_=stage[:]
+                out=wg_codes[(b, a)][:, lo:hi].bitcast(FP8X4),
+                scales=wg_plane[(b, a)][:, lo:hi],
+                in_=stage[:, PACK * lo : PACK * hi],
             )
 
         h_codes = {(c, b): held([P, CHUNK], U32, "h_codes%d%d" % (c, b)) for c in range(CHUNKS) for b in range(2)}
@@ -185,8 +185,8 @@ def tile_list_gmlpt_silu_gate_kernel(
                 for a in range(2):
                     nc.tensor.matmul_mx(
                         out=up[:, t, :],
-                        lhsT=wu[b][:, a, P * t : P * (t + 1)].bitcast(FP8X4),
-                        lhsT_scale=wu_plane[4 * a :, PASS * b + P * t : PASS * b + P * (t + 1)],
+                        lhsT=wu[b][:, t, a, :].bitcast(FP8X4),
+                        lhsT_scale=wu_plane[4 * a :, t, b, :],
                         rhs=words[(c, a)][:, cols].bitcast(FP8X4),
                         rhs_scale=planes[c][4 * a :, cols],
                         start=(a == 0),
@@ -264,15 +264,16 @@ def tile_list_gmlpt_silu_gate_kernel(
         gather_words(0, 0, 2)
         gather_plane(0, 2)
         permute_wu_plane()
-        cast_wg(0, 0, staging[0], 0, 1)
-        cast_wg(0, 1, staging[1], 0, 1)
+        for a in range(2):
+            for half in range(2):
+                cast_wg(0, a, staging[a], half)
         gather_words(2, 0, 2)
-        quantise_wg(0, 0, staging[0])
+        quantise_wg(0, 0, staging[0], 0, PASS)
         for c in range(2):
             for t in range(PACK):
                 gate_pass(c, 0, t, 0, banks[4 * c + t])
         gather_plane(2)
-        quantise_wg(0, 1, staging[1])
+        quantise_wg(0, 1, staging[1], 0, PASS)
         gather_words(0, 1)
         act0 = gate_part(0, 0, 0, (1,))
         gather_words(1, 1)
@@ -280,32 +281,31 @@ def tile_list_gmlpt_silu_gate_kernel(
         permute_wu(0)
         gather_words(2, 1)
         up_part(0, 0, act0, 0, staging[2])
+        gather_plane(3)
         quantise_h(0, 0, staging[2], 0, CHUNK)
         up_part(1, 0, act1, 4, staging[3])
-        cast_wg(1, 0, staging[2], 0, 2)
+        cast_wg(1, 0, late_stage, 0)
+        cast_wg(1, 0, late_stage, 1)
         act = gate_part(2, 0, 0, (0, 1))
-        cast_wg(1, 0, staging[2], 1, 2)
-        gather_plane(3)
-        quantise_h(1, 0, staging[3], 0, CHUNK)
+        cast_wg(1, 1, staging[2], 0)
         gather_words(3, 1)
+        quantise_h(1, 0, staging[3], 0, CHUNK)
+        quantise_wg(1, 0, late_stage, 0, PASS)
         up_part(2, 0, act, 4, staging[0])
-        cast_wg(1, 1, staging[3], 0, 2)
         act = gate_part(3, 0, 0, (0, 1))
-        cast_wg(1, 1, staging[3], 1, 2)
-        quantise_wg(1, 0, staging[2])
-        quantise_h(2, 0, staging[0], 0, CHUNK)
+        cast_wg(1, 1, staging[2], 1)
         permute_wu(1)
+        quantise_h(2, 0, staging[0], 0, CHUNK)
+        quantise_wg(1, 1, staging[2], 0, PASS // 2)
         for q in range(PACK):
             up_quarter(3, 0, q, act, banks[4 + q], staging[1])
             if q == 1:
-                quantise_wg(1, 1, staging[3])
+                quantise_wg(1, 1, staging[2], PASS // 2, PASS)
         act = gate_part(0, 1, 0, (0, 1))
-        pick_gate(2, 0)
+        pick_gate(3, 0)
         quantise_h(3, 0, staging[1], 0, CHUNK)
         up_part(0, 1, act, 4, staging[0])
         quantise_h(0, 1, staging[0], 0, CHUNK)
-        pick_gate(3, 0)
-        pick_gate(2, 1)
         pick_gate(3, 1)
         for c in (1, 2):
             act = gate_part(c, 1, 0, (0, 1))
@@ -315,14 +315,14 @@ def tile_list_gmlpt_silu_gate_kernel(
             gate_and_store(c - 1, 0, sums[0])
             gate_and_store(c - 1, 1, sums[1])
         act = gate_part(3, 1, 0, (0, 1))
-        for nt in range(2):
-            down(2, nt, slice(0, CHUNK), banks[4 + nt][:])
-            scale_and_store(2, nt, banks[4 + nt])
+        sums = down_chunk(2)
         for q in range(PACK + 1):
             if q < PACK:
-                up_quarter(3, 1, q, act, banks[4 + (q + 2) % 4], staging[3])
+                up_quarter(3, 1, q, act, banks[4 + q], staging[3])
             if q >= 1:
                 quantise_h(3, 1, staging[3], QUARTER * (q - 1), QUARTER * q)
+            if q in (1, 4):
+                gate_and_store(2, q // 4, sums[q // 4])
         for q in range(PACK):
             down_quarter(3, q)
             scale_and_store_quarter(3, q)

@@ -54,11 +54,6 @@ def tile_list_gmlpt_silu_gate_kernel(
                 )
             return plane
 
-        warm = held([P, 16], F32, "warm")
-        warm_out = held([P, 16], F32, "warm_out")
-        nc.vector.memset(warm[:], 0.0)
-        nc.scalar.activation(out=warm_out[:], in_=warm[:], func=SILU)
-
         wu_raw = [held([P, 2, PASS], I32, "wu_raw%d" % b) for b in range(2)]
 
         def load_wu(b):
@@ -67,35 +62,41 @@ def tile_list_gmlpt_silu_gate_kernel(
 
         wg_raw = {}
 
-        def load_wg(b, a):
-            raw = held([P, PACK, PASS], F32, "wg_raw%d%d" % (b, a))
-            nc.sync.dma_start(
-                out=raw[:],
-                in_=wg[PASS * a : PASS * (a + 1), PASS * b : PASS * (b + 1)].rearrange("(p j) c -> p j c", j=PACK),
-            )
-            wg_raw[(b, a)] = raw
+        def load_wg(b, a, parts):
+            rows = wg[PASS * a : PASS * (a + 1), PASS * b : PASS * (b + 1)].rearrange("(p j) c -> p j c", j=PACK)
+            width = PASS // parts
+            for part in range(parts):
+                raw = held([P, PACK, width], F32, "wg_raw%d%d%d" % (b, a, part))
+                nc.sync.dma_start(out=raw[:], in_=rows[:, :, width * part : width * (part + 1)])
+                wg_raw[(b, a, part)] = raw
 
         gate = [held([P, T], F32, "gate%d" % nt) for nt in range(2)]
 
-        load_tab(0)
-        nc.sync.dma_start(offsets[:], offs)
         tab_plane = held([P, T // 4], I32, "tab_plane")
+        load_wu(0)
+        nc.sync.dma_start(offsets[:], offs)
         for r in range(4):
-            nc.sync.dma_start(
+            queue = nc.scalar if r < 2 else nc.sync
+            queue.dma_start(
                 out=tab_plane[r:104:4, :],
                 in_=tab_scales[:, r : r + 13, :].rearrange("a u t -> u a t").bitcast(I32),
             )
         nc.sync.dma_start(
             out=tab_plane[104:, :], in_=tab_scales.rearrange("a q t -> (a q) t")[:24, :].bitcast(I32)
         )
-        load_wg(0, 0)
+        warm = held([P, 16], F32, "warm")
+        warm_out = held([P, 16], F32, "warm_out")
+        nc.vector.memset(warm[:], 0.0)
+        nc.scalar.activation(out=warm_out[:], in_=warm[:], func=SILU)
+
+        load_tab(0)
+        load_wg(0, 0, 1)
         wu_plane_raw = load_scales(nc.sync, wu_scales, R, "wu_plane_raw")
-        load_wg(0, 1)
+        load_wg(0, 1, 1)
         load_tab(1)
-        load_wu(0)
         load_wu(1)
-        load_wg(1, 0)
-        load_wg(1, 1)
+        load_wg(1, 0, 1)
+        load_wg(1, 1, 1)
         for nt in range(2):
             nc.sync.dma_start(out=gate[nt][:], in_=gT[P * nt : P * (nt + 1), :])
         wd_plane = load_scales(nc.sync, wd_scales, N, "wd_plane")
@@ -138,16 +139,24 @@ def tile_list_gmlpt_silu_gate_kernel(
             )
 
         staging = [held([P, PACK * PASS], BF16, "staging%d" % i) for i in range(4)]
-        late_stage = keep.tile([P, PACK * PASS], BF16, name="late_stage", tag="wu_raw0", align_bytes=64)
+        late_tile = keep.tile([P, 2, PACK * PASS], BF16, name="late_stage", tag="wu_raw1", align_bytes=64)
+        late_stage = [late_tile[:, a, :] for a in range(2)]
         wg_codes = {(b, a): held([P, PASS], U32, "wg_codes%d%d" % (b, a)) for b in range(2) for a in range(2)}
         wg_plane = {(b, a): held([P, PASS], U8, "wg_plane%d%d" % (b, a)) for b in range(2) for a in range(2)}
 
-        def cast_wg(b, a, stage, half):
-            pair = slice(2 * half, 2 * half + 2)
-            nc.scalar.copy(
-                out=stage[:].rearrange("p (t m j) -> p m t j", t=PACK, j=PACK)[:, :, pair],
-                in_=wg_raw[(b, a)][:].rearrange("p j (m t) -> p m t j", t=PACK)[:, :, pair],
-            )
+        def cast_views(b, a, part, stage):
+            src = wg_raw[(b, a, part)][:].rearrange("p j (m t) -> p m t j", t=PACK)
+            count = src.shape[1]
+            dst = stage[:].rearrange("p (t m j) -> p m t j", t=PACK, j=PACK)
+            return dst[:, count * part : count * (part + 1)], src
+
+        def cast_wg(b, a, part, stage, pair):
+            dst, src = cast_views(b, a, part, stage)
+            nc.scalar.copy(out=dst[:, :, 2 * pair : 2 * pair + 2], in_=src[:, :, 2 * pair : 2 * pair + 2])
+
+        def cast_wg_on_vector(b, a, part, stage):
+            dst, src = cast_views(b, a, part, stage)
+            nc.vector.tensor_copy(out=dst, in_=src)
 
         def quantise_wg(b, a, stage, lo, hi):
             nc.vector.quantize_mx(
@@ -170,21 +179,26 @@ def tile_list_gmlpt_silu_gate_kernel(
                 stop=(a == 1),
             )
 
+        def gate_rows(c, b, t, act, bank, passes):
+            for a in passes:
+                gate_pass(c, b, t, a, bank)
+            nc.scalar.activation(out=act[:, t, :], in_=bank[:], func=SILU)
+
         def gate_part(c, b, first_bank, passes):
             act = ring.tile([P, PACK, CHUNK], F32, name="act")
             for t in range(PACK):
-                for a in passes:
-                    gate_pass(c, b, t, a, banks[first_bank + t])
-                nc.scalar.activation(out=act[:, t, :], in_=banks[first_bank + t][:], func=SILU)
+                gate_rows(c, b, t, act, banks[first_bank + t], passes)
             return act
 
-        def up_quarter(c, b, q, act, bank, stage):
+        def up_view(bank):
+            return bank[:].rearrange("p (t n) -> p t n", t=PACK)
+
+        def up_sums(c, b, q, bank):
             cols = slice(QUARTER * q, QUARTER * (q + 1))
-            up = bank[:].rearrange("p (t n) -> p t n", t=PACK)
             for t in range(PACK):
                 for a in range(2):
                     nc.tensor.matmul_mx(
-                        out=up[:, t, :],
+                        out=up_view(bank)[:, t, :],
                         lhsT=wu[b][:, t, a, :].bitcast(FP8X4),
                         lhsT_scale=wu_plane[4 * a :, t, b, :],
                         rhs=words[(c, a)][:, cols].bitcast(FP8X4),
@@ -192,12 +206,18 @@ def tile_list_gmlpt_silu_gate_kernel(
                         start=(a == 0),
                         stop=(a == 1),
                     )
+
+        def multiply(q, act, bank, stage):
             nc.vector.tensor_tensor(
                 out=stage[:, PASS * q : PASS * (q + 1)].rearrange("p (n i t) -> p n t i", i=2, t=PACK),
-                in0=up.rearrange("p t (n i) -> p n t i", i=2),
-                in1=act[:, :, cols].rearrange("p t (n i) -> p n t i", i=2),
+                in0=up_view(bank).rearrange("p t (n i) -> p n t i", i=2),
+                in1=act[:, :, QUARTER * q : QUARTER * (q + 1)].rearrange("p t (n i) -> p n t i", i=2),
                 op=MULT,
             )
+
+        def up_quarter(c, b, q, act, bank, stage):
+            up_sums(c, b, q, bank)
+            multiply(q, act, bank, stage)
 
         def up_part(c, b, act, first_bank, stage):
             for q in range(PACK):
@@ -236,13 +256,11 @@ def tile_list_gmlpt_silu_gate_kernel(
             nc.vector.tensor_tensor(out=res[:], in0=gate[nt][:].indirect(chunk_list(c)), in1=y[:], op=MULT)
             nc.sync.dma_start(out=out[P * nt : P * (nt + 1), CHUNK * c : CHUNK * (c + 1)], in_=res[:])
 
-        def pick_gate(c, nt):
-            nc.vector.tensor_copy(out=picked[c][:, nt, :], in_=gate[nt][:].indirect(chunk_list(c)))
 
-        def scale_and_store(c, nt, bank):
-            res = held([P, CHUNK], F32, "res_late%d" % nt)
-            nc.vector.tensor_tensor(out=res[:], in0=bank[:], in1=picked[c][:, nt, :], op=MULT)
-            nc.sync.dma_start(out=out[P * nt : P * (nt + 1), CHUNK * c : CHUNK * (c + 1)], in_=res[:])
+        picked = wg_raw[(1, 1, 0)][:, 0:2, :]
+
+        def pick_gate(c, nt):
+            nc.vector.tensor_copy(out=picked[:, nt, :], in_=gate[nt][:].indirect(chunk_list(c)))
 
         def quarter_view(q):
             return banks[q][:, : 2 * QUARTER].rearrange("p (nt n) -> p nt n", nt=2)
@@ -254,75 +272,76 @@ def tile_list_gmlpt_silu_gate_kernel(
         def scale_and_store_quarter(c, q):
             res = held([P, 2, QUARTER], F32, "res_last%d" % q)
             nc.vector.tensor_tensor(
-                out=res[:], in0=quarter_view(q), in1=picked[c][:, :, QUARTER * q : QUARTER * (q + 1)], op=MULT
+                out=res[:], in0=quarter_view(q), in1=picked[:, :, QUARTER * q : QUARTER * (q + 1)], op=MULT
             )
             c0 = CHUNK * c + QUARTER * q
             nc.sync.dma_start(out=out[:, c0 : c0 + QUARTER].rearrange("(nt p) j -> p nt j", p=P), in_=res[:])
 
-        picked = {2: wg_raw[(1, 1)][:, 0:2, :], 3: wg_raw[(1, 1)][:, 2:4, :]}
-
+        permute_wu(0)
+        gather_plane(0, 4)
         gather_words(0, 0, 2)
-        gather_plane(0, 2)
-        permute_wu_plane()
-        for a in range(2):
-            for half in range(2):
-                cast_wg(0, a, staging[a], half)
         gather_words(2, 0, 2)
+        for a in range(2):
+            for pair in range(2):
+                cast_wg(0, a, 0, staging[a], pair)
+        permute_wu_plane()
         quantise_wg(0, 0, staging[0], 0, PASS)
         for c in range(2):
             for t in range(PACK):
                 gate_pass(c, 0, t, 0, banks[4 * c + t])
-        gather_plane(2)
         quantise_wg(0, 1, staging[1], 0, PASS)
         gather_words(0, 1)
         act0 = gate_part(0, 0, 0, (1,))
         gather_words(1, 1)
         act1 = gate_part(1, 0, 4, (1,))
-        permute_wu(0)
+        permute_wu(1)
         gather_words(2, 1)
         up_part(0, 0, act0, 0, staging[2])
-        gather_plane(3)
-        quantise_h(0, 0, staging[2], 0, CHUNK)
-        up_part(1, 0, act1, 4, staging[3])
-        cast_wg(1, 0, late_stage, 0)
-        cast_wg(1, 0, late_stage, 1)
-        act = gate_part(2, 0, 0, (0, 1))
-        cast_wg(1, 1, staging[2], 0)
         gather_words(3, 1)
-        quantise_h(1, 0, staging[3], 0, CHUNK)
-        quantise_wg(1, 0, late_stage, 0, PASS)
-        up_part(2, 0, act, 4, staging[0])
-        act = gate_part(3, 0, 0, (0, 1))
-        cast_wg(1, 1, staging[2], 1)
-        permute_wu(1)
-        quantise_h(2, 0, staging[0], 0, CHUNK)
-        quantise_wg(1, 1, staging[2], 0, PASS // 2)
+        act = act1
+        cast_wg(1, 0, 0, late_stage[0], 0)
+        cast_wg(1, 1, 0, late_stage[1], 0)
         for q in range(PACK):
-            up_quarter(3, 0, q, act, banks[4 + q], staging[1])
-            if q == 1:
-                quantise_wg(1, 1, staging[2], PASS // 2, PASS)
-        act = gate_part(0, 1, 0, (0, 1))
+            up_quarter(1, 0, q, act, banks[4 + q], staging[3])
+            if q == 0:
+                quantise_h(0, 0, staging[2], 0, CHUNK)
+        act = gate_part(2, 0, 0, (0, 1))
+        cast_wg(1, 0, 0, late_stage[0], 1)
+        cast_wg(1, 1, 0, late_stage[1], 1)
+        for a in range(2):
+            quantise_wg(1, a, late_stage[a], 0, PASS // 2)
+        quantise_h(1, 0, staging[3], 0, CHUNK)
+        up_part(2, 0, act, 4, staging[2])
+        act = ring.tile([P, PACK, CHUNK], F32, name="act")
+        for pair in range(2):
+            if pair == 1:
+                for a in range(2):
+                    quantise_wg(1, a, late_stage[a], PASS // 2, PASS)
+            for t in (2 * pair, 2 * pair + 1):
+                gate_rows(0, 1, t, act, banks[t], (0, 1))
+            for q in (2 * pair, 2 * pair + 1):
+                up_sums(0, 1, q, banks[4 + q])
+        quantise_h(2, 0, staging[2], 0, CHUNK)
         pick_gate(3, 0)
-        quantise_h(3, 0, staging[1], 0, CHUNK)
-        up_part(0, 1, act, 4, staging[0])
-        quantise_h(0, 1, staging[0], 0, CHUNK)
+        for q in range(PACK):
+            multiply(q, act, banks[4 + q], staging[0])
         pick_gate(3, 1)
-        for c in (1, 2):
-            act = gate_part(c, 1, 0, (0, 1))
-            sums = down_chunk(c - 1)
-            up_part(c, 1, act, 4, staging[c])
-            quantise_h(c, 1, staging[c], 0, CHUNK)
-            gate_and_store(c - 1, 0, sums[0])
-            gate_and_store(c - 1, 1, sums[1])
+        quantise_h(0, 1, staging[0], 0, CHUNK)
+        for u, (c, b) in enumerate(((1, 1), (2, 1), (3, 0))):
+            act = gate_part(c, b, 0, (0, 1))
+            for q in range(PACK):
+                up_quarter(c, b, q, act, banks[4 + q], staging[u + 1])
+                if q == 2:
+                    sums = down_chunk(u)
+            gate_and_store(u, 0, sums[0])
+            quantise_h(c, b, staging[u + 1], 0, CHUNK)
+            gate_and_store(u, 1, sums[1])
         act = gate_part(3, 1, 0, (0, 1))
-        sums = down_chunk(2)
         for q in range(PACK + 1):
             if q < PACK:
-                up_quarter(3, 1, q, act, banks[4 + q], staging[3])
+                up_quarter(3, 1, q, act, banks[4 + q], staging[0])
             if q >= 1:
-                quantise_h(3, 1, staging[3], QUARTER * (q - 1), QUARTER * q)
-            if q in (1, 4):
-                gate_and_store(2, q // 4, sums[q // 4])
+                quantise_h(3, 1, staging[0], QUARTER * (q - 1), QUARTER * q)
         for q in range(PACK):
             down_quarter(3, q)
             scale_and_store_quarter(3, q)

@@ -20,8 +20,12 @@ PACK = 4
 PASS = P * PACK
 CHUNK = 512
 CHUNKS = J // CHUNK
+LAST = CHUNKS - 1
 QUARTER = CHUNK // PACK
 LIST_COLS = CHUNK // 16
+UP = 4
+STEPPED_ROWS = 13
+STEPPED_END = 8 * STEPPED_ROWS
 
 
 def tile_list_gmlpt_silu_gate_kernel(
@@ -44,11 +48,11 @@ def tile_list_gmlpt_silu_gate_kernel(
         def load_tab(a):
             nc.sync.dma_start(out=tab[a][:], in_=tab_words[a].rearrange("p t i -> p (t i)").bitcast(I32))
 
-        def load_scales(queue, dram, width, name):
+        def load_scales(dram, width, name):
             plane = held([P, width // 4], I32, name)
             nc.vector.memset(plane[:], 0)
             for quad in range(4):
-                queue.dma_start(
+                nc.sync.dma_start(
                     out=plane[32 * quad : 32 * quad + 8, :],
                     in_=dram[:, 4 * quad : 4 * quad + 4, :].bitcast(I32),
                 )
@@ -62,44 +66,43 @@ def tile_list_gmlpt_silu_gate_kernel(
 
         wg_raw = {}
 
-        def load_wg(b, a, parts):
+        def load_wg(b, a):
             rows = wg[PASS * a : PASS * (a + 1), PASS * b : PASS * (b + 1)].rearrange("(p j) c -> p j c", j=PACK)
-            width = PASS // parts
-            for part in range(parts):
-                raw = held([P, PACK, width], F32, "wg_raw%d%d%d" % (b, a, part))
-                nc.sync.dma_start(out=raw[:], in_=rows[:, :, width * part : width * (part + 1)])
-                wg_raw[(b, a, part)] = raw
+            wg_raw[(b, a)] = held([P, PACK, PASS], F32, "wg_raw%d%d" % (b, a))
+            nc.sync.dma_start(out=wg_raw[(b, a)][:], in_=rows)
 
         gate = [held([P, T], F32, "gate%d" % nt) for nt in range(2)]
 
         tab_plane = held([P, T // 4], I32, "tab_plane")
-        load_wu(0)
         nc.sync.dma_start(offsets[:], offs)
         for r in range(4):
             queue = nc.scalar if r < 2 else nc.sync
             queue.dma_start(
-                out=tab_plane[r:104:4, :],
-                in_=tab_scales[:, r : r + 13, :].rearrange("a u t -> u a t").bitcast(I32),
+                out=tab_plane[r:STEPPED_END:4, :],
+                in_=tab_scales[:, r : r + STEPPED_ROWS, :].rearrange("a u t -> u a t").bitcast(I32),
             )
-        nc.sync.dma_start(
-            out=tab_plane[104:, :], in_=tab_scales.rearrange("a q t -> (a q) t")[:24, :].bitcast(I32)
-        )
+        for lo, hi in ((STEPPED_END, P - 16), (P - 16, P)):
+            nc.sync.dma_start(
+                out=tab_plane[lo:hi, :], in_=tab_scales.rearrange("a q t -> (a q) t")[: hi - lo, :].bitcast(I32)
+            )
+
         warm = held([P, 16], F32, "warm")
         warm_out = held([P, 16], F32, "warm_out")
         nc.vector.memset(warm[:], 0.0)
         nc.scalar.activation(out=warm_out[:], in_=warm[:], func=SILU)
 
         load_tab(0)
-        load_wg(0, 0, 1)
-        wu_plane_raw = load_scales(nc.sync, wu_scales, R, "wu_plane_raw")
-        load_wg(0, 1, 1)
+        load_wg(0, 0)
+        wu_plane_raw = load_scales(wu_scales, R, "wu_plane_raw")
+        load_wg(0, 1)
         load_tab(1)
+        load_wu(0)
         load_wu(1)
-        load_wg(1, 0, 1)
-        load_wg(1, 1, 1)
+        load_wg(1, 0)
+        load_wg(1, 1)
         for nt in range(2):
             nc.sync.dma_start(out=gate[nt][:], in_=gT[P * nt : P * (nt + 1), :])
-        wd_plane = load_scales(nc.sync, wd_scales, N, "wd_plane")
+        wd_plane = load_scales(wd_scales, N, "wd_plane")
         wd = held([P, 2, N], I32, "wd")
         nc.sync.dma_start(out=wd[:], in_=wd_words.rearrange("a p n i -> p a (n i)").bitcast(I32))
 
@@ -107,19 +110,18 @@ def tile_list_gmlpt_silu_gate_kernel(
             return offsets[:, LIST_COLS * c : LIST_COLS * (c + count)]
 
         words = {}
-        planes = {}
 
-        def gather_words(c, a, count=1):
-            picked_words = held([P, CHUNK * count], U32, "words%d%d" % (c, a))
+        def gather_words(c, a, count=1, tag=""):
+            picked_words = keep.tile([P, CHUNK * count], U32, name="words%d%d" % (c, a), tag=tag, align_bytes=64)
             nc.vector.tensor_copy(out=picked_words[:], in_=tab[a][:].bitcast(U32).indirect(chunk_list(c, count)))
             for i in range(count):
                 words[(c + i, a)] = picked_words[:, CHUNK * i : CHUNK * (i + 1)]
 
-        def gather_plane(c, count=1):
-            picked_plane = held([P, CHUNK * count], U8, "plane%d" % c)
-            nc.vector.tensor_copy(out=picked_plane[:], in_=tab_plane[:].bitcast(U8).indirect(chunk_list(c, count)))
-            for i in range(count):
-                planes[c + i] = picked_plane[:, CHUNK * i : CHUNK * (i + 1)]
+        picked_plane = held([P, J], U8, "picked_plane")
+        planes = [picked_plane[:, CHUNK * c : CHUNK * (c + 1)] for c in range(CHUNKS)]
+
+        def gather_plane():
+            nc.vector.tensor_copy(out=picked_plane[:], in_=tab_plane[:].bitcast(U8).indirect(chunk_list(0, CHUNKS)))
 
         wu = {}
 
@@ -144,19 +146,10 @@ def tile_list_gmlpt_silu_gate_kernel(
         wg_codes = {(b, a): held([P, PASS], U32, "wg_codes%d%d" % (b, a)) for b in range(2) for a in range(2)}
         wg_plane = {(b, a): held([P, PASS], U8, "wg_plane%d%d" % (b, a)) for b in range(2) for a in range(2)}
 
-        def cast_views(b, a, part, stage):
-            src = wg_raw[(b, a, part)][:].rearrange("p j (m t) -> p m t j", t=PACK)
-            count = src.shape[1]
+        def cast_wg(b, a, stage, pair):
+            src = wg_raw[(b, a)][:].rearrange("p j (m t) -> p m t j", t=PACK)
             dst = stage[:].rearrange("p (t m j) -> p m t j", t=PACK, j=PACK)
-            return dst[:, count * part : count * (part + 1)], src
-
-        def cast_wg(b, a, part, stage, pair):
-            dst, src = cast_views(b, a, part, stage)
             nc.scalar.copy(out=dst[:, :, 2 * pair : 2 * pair + 2], in_=src[:, :, 2 * pair : 2 * pair + 2])
-
-        def cast_wg_on_vector(b, a, part, stage):
-            dst, src = cast_views(b, a, part, stage)
-            nc.vector.tensor_copy(out=dst, in_=src)
 
         def quantise_wg(b, a, stage, lo, hi):
             nc.vector.quantize_mx(
@@ -231,15 +224,15 @@ def tile_list_gmlpt_silu_gate_kernel(
             )
 
         def down(c, nt, cols, acc):
-            for a in range(2):
+            for b in range(2):
                 nc.tensor.matmul_mx(
                     out=acc,
-                    lhsT=wd[:, a, P * nt : P * (nt + 1)].bitcast(FP8X4),
-                    lhsT_scale=wd_plane[:].bitcast(U8)[4 * a :, P * nt : P * (nt + 1)],
-                    rhs=h_codes[(c, a)][:, cols].bitcast(FP8X4),
-                    rhs_scale=h_plane[(c, a)][:, cols],
-                    start=(a == 0),
-                    stop=(a == 1),
+                    lhsT=wd[:, b, P * nt : P * (nt + 1)].bitcast(FP8X4),
+                    lhsT_scale=wd_plane[:].bitcast(U8)[4 * b :, P * nt : P * (nt + 1)],
+                    rhs=h_codes[(c, b)][:, cols].bitcast(FP8X4),
+                    rhs_scale=h_plane[(c, b)][:, cols],
+                    start=(b == 0),
+                    stop=(b == 1),
                 )
 
         def down_chunk(c):
@@ -256,62 +249,59 @@ def tile_list_gmlpt_silu_gate_kernel(
             nc.vector.tensor_tensor(out=res[:], in0=gate[nt][:].indirect(chunk_list(c)), in1=y[:], op=MULT)
             nc.sync.dma_start(out=out[P * nt : P * (nt + 1), CHUNK * c : CHUNK * (c + 1)], in_=res[:])
 
+        last_gates = wg_raw[(1, 1)][:, 0:2, :]
 
-        picked = wg_raw[(1, 1, 0)][:, 0:2, :]
-
-        def pick_gate(c, nt):
-            nc.vector.tensor_copy(out=picked[:, nt, :], in_=gate[nt][:].indirect(chunk_list(c)))
+        def pick_last_gates(nt):
+            nc.vector.tensor_copy(out=last_gates[:, nt, :], in_=gate[nt][:].indirect(chunk_list(LAST)))
 
         def quarter_view(q):
             return banks[q][:, : 2 * QUARTER].rearrange("p (nt n) -> p nt n", nt=2)
 
-        def down_quarter(c, q):
+        def finish_last_quarter(q):
+            cols = slice(QUARTER * q, QUARTER * (q + 1))
             for nt in range(2):
-                down(c, nt, slice(QUARTER * q, QUARTER * (q + 1)), quarter_view(q)[:, nt, :])
-
-        def scale_and_store_quarter(c, q):
+                down(LAST, nt, cols, quarter_view(q)[:, nt, :])
             res = held([P, 2, QUARTER], F32, "res_last%d" % q)
-            nc.vector.tensor_tensor(
-                out=res[:], in0=quarter_view(q), in1=picked[:, :, QUARTER * q : QUARTER * (q + 1)], op=MULT
-            )
-            c0 = CHUNK * c + QUARTER * q
+            nc.vector.tensor_tensor(out=res[:], in0=quarter_view(q), in1=last_gates[:, :, cols], op=MULT)
+            c0 = CHUNK * LAST + QUARTER * q
             nc.sync.dma_start(out=out[:, c0 : c0 + QUARTER].rearrange("(nt p) j -> p nt j", p=P), in_=res[:])
 
-        permute_wu(0)
-        gather_plane(0, 4)
+        gather_plane()
         gather_words(0, 0, 2)
         gather_words(2, 0, 2)
         for a in range(2):
             for pair in range(2):
-                cast_wg(0, a, 0, staging[a], pair)
+                cast_wg(0, a, staging[a], pair)
         permute_wu_plane()
         quantise_wg(0, 0, staging[0], 0, PASS)
         for c in range(2):
             for t in range(PACK):
-                gate_pass(c, 0, t, 0, banks[4 * c + t])
+                gate_pass(c, 0, t, 0, banks[PACK * c + t])
         quantise_wg(0, 1, staging[1], 0, PASS)
+
         gather_words(0, 1)
-        act0 = gate_part(0, 0, 0, (1,))
+        act_first = gate_part(0, 0, 0, (1,))
         gather_words(1, 1)
-        act1 = gate_part(1, 0, 4, (1,))
+        act = gate_part(1, 0, UP, (1,))
+        permute_wu(0)
+        gather_words(2, 1, 2, tag="wu_raw0")
+        up_part(0, 0, act_first, 0, staging[2])
         permute_wu(1)
-        gather_words(2, 1)
-        up_part(0, 0, act0, 0, staging[2])
-        gather_words(3, 1)
-        act = act1
-        cast_wg(1, 0, 0, late_stage[0], 0)
-        cast_wg(1, 1, 0, late_stage[1], 0)
+        for a in range(2):
+            cast_wg(1, a, late_stage[a], 0)
         for q in range(PACK):
-            up_quarter(1, 0, q, act, banks[4 + q], staging[3])
+            up_quarter(1, 0, q, act, banks[UP + q], staging[3])
             if q == 0:
                 quantise_h(0, 0, staging[2], 0, CHUNK)
+
         act = gate_part(2, 0, 0, (0, 1))
-        cast_wg(1, 0, 0, late_stage[0], 1)
-        cast_wg(1, 1, 0, late_stage[1], 1)
+        for a in range(2):
+            cast_wg(1, a, late_stage[a], 1)
         for a in range(2):
             quantise_wg(1, a, late_stage[a], 0, PASS // 2)
         quantise_h(1, 0, staging[3], 0, CHUNK)
-        up_part(2, 0, act, 4, staging[2])
+        up_part(2, 0, act, UP, staging[2])
+
         act = ring.tile([P, PACK, CHUNK], F32, name="act")
         for pair in range(2):
             if pair == 1:
@@ -320,28 +310,30 @@ def tile_list_gmlpt_silu_gate_kernel(
             for t in (2 * pair, 2 * pair + 1):
                 gate_rows(0, 1, t, act, banks[t], (0, 1))
             for q in (2 * pair, 2 * pair + 1):
-                up_sums(0, 1, q, banks[4 + q])
+                up_sums(0, 1, q, banks[UP + q])
         quantise_h(2, 0, staging[2], 0, CHUNK)
-        pick_gate(3, 0)
+        pick_last_gates(0)
         for q in range(PACK):
-            multiply(q, act, banks[4 + q], staging[0])
-        pick_gate(3, 1)
+            multiply(q, act, banks[UP + q], staging[0])
+        pick_last_gates(1)
         quantise_h(0, 1, staging[0], 0, CHUNK)
-        for u, (c, b) in enumerate(((1, 1), (2, 1), (3, 0))):
+
+        for done, (c, b) in enumerate(((1, 1), (2, 1), (LAST, 0))):
             act = gate_part(c, b, 0, (0, 1))
+            stage = staging[done + 1]
             for q in range(PACK):
-                up_quarter(c, b, q, act, banks[4 + q], staging[u + 1])
-                if q == 2:
-                    sums = down_chunk(u)
-            gate_and_store(u, 0, sums[0])
-            quantise_h(c, b, staging[u + 1], 0, CHUNK)
-            gate_and_store(u, 1, sums[1])
-        act = gate_part(3, 1, 0, (0, 1))
+                up_quarter(c, b, q, act, banks[UP + q], stage)
+                if q == PACK - 2:
+                    sums = down_chunk(done)
+            gate_and_store(done, 0, sums[0])
+            quantise_h(c, b, stage, 0, CHUNK)
+            gate_and_store(done, 1, sums[1])
+
+        act = gate_part(LAST, 1, 0, (0, 1))
         for q in range(PACK + 1):
             if q < PACK:
-                up_quarter(3, 1, q, act, banks[4 + q], staging[0])
+                up_quarter(LAST, 1, q, act, banks[UP + q], staging[0])
             if q >= 1:
-                quantise_h(3, 1, staging[0], QUARTER * (q - 1), QUARTER * q)
+                quantise_h(LAST, 1, staging[0], QUARTER * (q - 1), QUARTER * q)
         for q in range(PACK):
-            down_quarter(3, q)
-            scale_and_store_quarter(3, q)
+            finish_last_quarter(q)

@@ -64,26 +64,23 @@ def tile_list_gmlpt_silu_gate_kernel(
             rows = wu_words.rearrange("a p r i -> p a (r i)")
             nc.sync.dma_start(out=wu_raw[b][:], in_=rows[:, :, 4 * PASS * b : 4 * PASS * (b + 1)].bitcast(I32))
 
-        wg_raw = {}
+        wg_raw = {(b, a): held([P, PACK, PASS], F32, "wg_raw%d%d" % (b, a)) for b in range(2) for a in range(2)}
 
-        def load_wg(b, a):
+        def load_wg(b, a, lo=0, hi=PACK):
             rows = wg[PASS * a : PASS * (a + 1), PASS * b : PASS * (b + 1)].rearrange("(p j) c -> p j c", j=PACK)
-            wg_raw[(b, a)] = held([P, PACK, PASS], F32, "wg_raw%d%d" % (b, a))
-            nc.sync.dma_start(out=wg_raw[(b, a)][:], in_=rows)
+            nc.sync.dma_start(out=wg_raw[(b, a)][:, lo:hi, :], in_=rows[:, lo:hi, :])
 
         gate = [held([P, T], F32, "gate%d" % nt) for nt in range(2)]
 
         tab_plane = held([P, T // 4], I32, "tab_plane")
+        nc.vector.memset(tab_plane[96:, :], 0)
         nc.sync.dma_start(offsets[:], offs)
+        load_wg(0, 0)
         for r in range(4):
             queue = nc.scalar if r < 2 else nc.sync
             queue.dma_start(
                 out=tab_plane[r:STEPPED_END:4, :],
                 in_=tab_scales[:, r : r + STEPPED_ROWS, :].rearrange("a u t -> u a t").bitcast(I32),
-            )
-        for lo, hi in ((STEPPED_END, P - 16), (P - 16, P)):
-            nc.sync.dma_start(
-                out=tab_plane[lo:hi, :], in_=tab_scales.rearrange("a q t -> (a q) t")[: hi - lo, :].bitcast(I32)
             )
 
         warm = held([P, 16], F32, "warm")
@@ -92,8 +89,13 @@ def tile_list_gmlpt_silu_gate_kernel(
         nc.scalar.activation(out=warm_out[:], in_=warm[:], func=SILU)
 
         load_tab(0)
-        load_wg(0, 0)
-        wu_plane_raw = load_scales(wu_scales, R, "wu_plane_raw")
+        wu_plane_raw = held([P, R // 4], I32, "wu_plane_raw")
+        nc.vector.memset(wu_plane_raw[:], 0)
+        for r in range(4):
+            nc.sync.dma_start(
+                out=wu_plane_raw[r : 8 * 13 : 4, :],
+                in_=wu_scales[:, r : r + 13, :].rearrange("a u t -> u a t").bitcast(I32),
+            )
         load_wg(0, 1)
         load_tab(1)
         load_wu(0)
@@ -212,6 +214,16 @@ def tile_list_gmlpt_silu_gate_kernel(
             up_sums(c, b, q, bank)
             multiply(q, act, bank, stage)
 
+        def share_first_quarter(act, stage):
+            parked = ring.tile([P, QUARTER, PACK], F32, name="parked")
+            nc.scalar.copy(out=parked[:], in_=up_view(banks[UP]).rearrange("p t n -> p n t"))
+            nc.gpsimd.tensor_tensor(
+                out=stage[:, :PASS].rearrange("p (n t) -> p n t", t=PACK),
+                in0=parked[:],
+                in1=act[:, :, :QUARTER].rearrange("p t n -> p n t"),
+                op=MULT,
+            )
+
         def up_part(c, b, act, first_bank, stage):
             for q in range(PACK):
                 up_quarter(c, b, q, act, banks[first_bank + q], stage)
@@ -235,11 +247,14 @@ def tile_list_gmlpt_silu_gate_kernel(
                     stop=(b == 1),
                 )
 
-        def down_chunk(c):
+        def down_chunk(c, next_stage):
             sums = []
             for nt in range(2):
                 down(c, nt, slice(0, CHUNK), banks[nt][:])
-                y = ring.tile([P, CHUNK], F32, name="y")
+                if nt == 0:
+                    y = ring.tile([P, CHUNK], F32, name="y")
+                else:
+                    y = next_stage[:].bitcast(F32)[:, :CHUNK]
                 nc.scalar.copy(out=y[:], in_=banks[nt][:])
                 sums.append(y)
             return sums
@@ -267,13 +282,13 @@ def tile_list_gmlpt_silu_gate_kernel(
             nc.sync.dma_start(out=out[:, c0 : c0 + QUARTER].rearrange("(nt p) j -> p nt j", p=P), in_=res[:])
 
         gather_plane()
-        gather_words(0, 0, 2)
-        gather_words(2, 0, 2)
+        gather_words(0, 0)
         for a in range(2):
             for pair in range(2):
                 cast_wg(0, a, staging[a], pair)
-        permute_wu_plane()
         quantise_wg(0, 0, staging[0], 0, PASS)
+        gather_words(1, 0, 2, tag="wg_raw00")
+        permute_wu_plane()
         for c in range(2):
             for t in range(PACK):
                 gate_pass(c, 0, t, 0, banks[PACK * c + t])
@@ -284,7 +299,7 @@ def tile_list_gmlpt_silu_gate_kernel(
         gather_words(1, 1)
         act = gate_part(1, 0, UP, (1,))
         permute_wu(0)
-        gather_words(2, 1, 2, tag="wu_raw0")
+        gather_words(2, 1, tag="wu_raw0")
         up_part(0, 0, act_first, 0, staging[2])
         permute_wu(1)
         for a in range(2):
@@ -300,7 +315,10 @@ def tile_list_gmlpt_silu_gate_kernel(
         for a in range(2):
             quantise_wg(1, a, late_stage[a], 0, PASS // 2)
         quantise_h(1, 0, staging[3], 0, CHUNK)
-        up_part(2, 0, act, UP, staging[2])
+        up_sums(2, 0, 0, banks[UP])
+        share_first_quarter(act, staging[3])
+        for q in range(1, PACK):
+            up_quarter(2, 0, q, act, banks[UP + q], staging[3])
 
         act = ring.tile([P, PACK, CHUNK], F32, name="act")
         for pair in range(2):
@@ -311,20 +329,28 @@ def tile_list_gmlpt_silu_gate_kernel(
                 gate_rows(0, 1, t, act, banks[t], (0, 1))
             for q in (2 * pair, 2 * pair + 1):
                 up_sums(0, 1, q, banks[UP + q])
-        quantise_h(2, 0, staging[2], 0, CHUNK)
         pick_last_gates(0)
-        for q in range(PACK):
-            multiply(q, act, banks[UP + q], staging[0])
+        quantise_h(2, 0, staging[3], 0, CHUNK)
+        share_first_quarter(act, staging[3])
+        for q in range(1, PACK):
+            multiply(q, act, banks[UP + q], staging[3])
         pick_last_gates(1)
-        quantise_h(0, 1, staging[0], 0, CHUNK)
+        quantise_h(0, 1, staging[3], 0, CHUNK)
 
         for done, (c, b) in enumerate(((1, 1), (2, 1), (LAST, 0))):
             act = gate_part(c, b, 0, (0, 1))
-            stage = staging[done + 1]
+            stage = staging[(done + 3) % 4]
             for q in range(PACK):
-                up_quarter(c, b, q, act, banks[UP + q], stage)
+                up_sums(c, b, q, banks[UP + q])
+                if q == 0:
+                    share_first_quarter(act, stage)
+                else:
+                    multiply(q, act, banks[UP + q], stage)
                 if q == PACK - 2:
-                    sums = down_chunk(done)
+                    sums = down_chunk(done, staging[done])
+                    if done == 0:
+                        gather_words(LAST, 0, tag="wg_raw10")
+                        gather_words(LAST, 1, tag="wu_raw1")
             gate_and_store(done, 0, sums[0])
             quantise_h(c, b, stage, 0, CHUNK)
             gate_and_store(done, 1, sums[1])
@@ -332,8 +358,24 @@ def tile_list_gmlpt_silu_gate_kernel(
         act = gate_part(LAST, 1, 0, (0, 1))
         for q in range(PACK + 1):
             if q < PACK:
-                up_quarter(LAST, 1, q, act, banks[UP + q], staging[0])
+                up_quarter(LAST, 1, q, act, banks[UP + q], staging[2])
             if q >= 1:
-                quantise_h(LAST, 1, staging[0], QUARTER * (q - 1), QUARTER * q)
-        for q in range(PACK):
+                quantise_h(LAST, 1, staging[2], QUARTER * (q - 1), QUARTER * q)
+        for q in range(PACK - 1):
             finish_last_quarter(q)
+        cols = slice(CHUNK - QUARTER, CHUNK)
+        for b in range(2):
+            for nt in range(2):
+                nc.tensor.matmul_mx(
+                    out=banks[PACK - 1 + nt][:, :QUARTER],
+                    lhsT=wd[:, b, P * nt : P * (nt + 1)].bitcast(FP8X4),
+                    lhsT_scale=wd_plane[:].bitcast(U8)[4 * b :, P * nt : P * (nt + 1)],
+                    rhs=h_codes[(LAST, b)][:, cols].bitcast(FP8X4),
+                    rhs_scale=h_plane[(LAST, b)][:, cols],
+                    start=(b == 0),
+                    stop=(b == 1),
+                )
+        for nt, queue in enumerate((nc.scalar, nc.sync)):
+            res = held([P, QUARTER], F32, "res_end%d" % nt)
+            nc.vector.tensor_tensor(out=res[:], in0=banks[PACK - 1 + nt][:, :QUARTER], in1=last_gates[:, nt, cols], op=MULT)
+            queue.dma_start(out=out[P * nt : P * (nt + 1), J - QUARTER :], in_=res[:])

@@ -202,8 +202,8 @@ def tile_list_gmlpt_silu_gate_kernel(
                         stop=(a == 1),
                     )
 
-        def multiply(q, act, bank, stage):
-            nc.vector.tensor_tensor(
+        def multiply(q, act, bank, stage, engine=nc.vector):
+            engine.tensor_tensor(
                 out=stage[:, PASS * q : PASS * (q + 1)].rearrange("p (n i t) -> p n t i", i=2, t=PACK),
                 in0=up_view(bank).rearrange("p t (n i) -> p n t i", i=2),
                 in1=act[:, :, QUARTER * q : QUARTER * (q + 1)].rearrange("p t (n i) -> p n t i", i=2),
@@ -215,14 +215,9 @@ def tile_list_gmlpt_silu_gate_kernel(
             multiply(q, act, bank, stage)
 
         def share_first_quarter(act, stage):
-            parked = ring.tile([P, QUARTER, PACK], F32, name="parked")
-            nc.scalar.copy(out=parked[:], in_=up_view(banks[UP]).rearrange("p t n -> p n t"))
-            nc.gpsimd.tensor_tensor(
-                out=stage[:, :PASS].rearrange("p (n t) -> p n t", t=PACK),
-                in0=parked[:],
-                in1=act[:, :, :QUARTER].rearrange("p t n -> p n t"),
-                op=MULT,
-            )
+            parked = ring.tile([P, CHUNK], F32, name="parked")
+            nc.scalar.copy(out=parked[:], in_=banks[UP][:])
+            multiply(0, act, parked, stage, nc.gpsimd)
 
         def up_part(c, b, act, first_bank, stage):
             for q in range(PACK):

@@ -66,16 +66,18 @@ def tile_list_gmlpt_silu_gate_kernel(
 
         wg_raw = {(b, a): held([P, PACK, PASS], F32, "wg_raw%d%d" % (b, a)) for b in range(2) for a in range(2)}
 
-        def load_wg(b, a, lo=0, hi=PACK):
+        def load_wg(b, a):
             rows = wg[PASS * a : PASS * (a + 1), PASS * b : PASS * (b + 1)].rearrange("(p j) c -> p j c", j=PACK)
-            nc.sync.dma_start(out=wg_raw[(b, a)][:, lo:hi, :], in_=rows[:, lo:hi, :])
+            nc.sync.dma_start(out=wg_raw[(b, a)][:], in_=rows)
 
         gate = [held([P, T], F32, "gate%d" % nt) for nt in range(2)]
 
         tab_plane = held([P, T // 4], I32, "tab_plane")
-        nc.vector.memset(tab_plane[96:, :], 0)
         nc.sync.dma_start(offsets[:], offs)
-        load_wg(0, 0)
+        for lo, hi in ((STEPPED_END, P - 16), (P - 16, P)):
+            nc.sync.dma_start(
+                out=tab_plane[lo:hi, :], in_=tab_scales.rearrange("a q t -> (a q) t")[: hi - lo, :].bitcast(I32)
+            )
         for r in range(4):
             queue = nc.scalar if r < 2 else nc.sync
             queue.dma_start(
@@ -89,13 +91,8 @@ def tile_list_gmlpt_silu_gate_kernel(
         nc.scalar.activation(out=warm_out[:], in_=warm[:], func=SILU)
 
         load_tab(0)
-        wu_plane_raw = held([P, R // 4], I32, "wu_plane_raw")
-        nc.vector.memset(wu_plane_raw[:], 0)
-        for r in range(4):
-            nc.sync.dma_start(
-                out=wu_plane_raw[r : 8 * 13 : 4, :],
-                in_=wu_scales[:, r : r + 13, :].rearrange("a u t -> u a t").bitcast(I32),
-            )
+        load_wg(0, 0)
+        wu_plane_raw = load_scales(wu_scales, R, "wu_plane_raw")
         load_wg(0, 1)
         load_tab(1)
         load_wu(0)
@@ -202,10 +199,10 @@ def tile_list_gmlpt_silu_gate_kernel(
                         stop=(a == 1),
                     )
 
-        def multiply(q, act, bank, stage, engine=nc.vector):
+        def multiply(q, act, up, stage, engine=nc.vector):
             engine.tensor_tensor(
                 out=stage[:, PASS * q : PASS * (q + 1)].rearrange("p (n i t) -> p n t i", i=2, t=PACK),
-                in0=up_view(bank).rearrange("p t (n i) -> p n t i", i=2),
+                in0=up_view(up).rearrange("p t (n i) -> p n t i", i=2),
                 in1=act[:, :, QUARTER * q : QUARTER * (q + 1)].rearrange("p t (n i) -> p n t i", i=2),
                 op=MULT,
             )
@@ -230,17 +227,20 @@ def tile_list_gmlpt_silu_gate_kernel(
                 in_=stage[:, PACK * lo : PACK * hi],
             )
 
+        def down_pass(c, b, nt, cols, acc):
+            nc.tensor.matmul_mx(
+                out=acc,
+                lhsT=wd[:, b, P * nt : P * (nt + 1)].bitcast(FP8X4),
+                lhsT_scale=wd_plane[:].bitcast(U8)[4 * b :, P * nt : P * (nt + 1)],
+                rhs=h_codes[(c, b)][:, cols].bitcast(FP8X4),
+                rhs_scale=h_plane[(c, b)][:, cols],
+                start=(b == 0),
+                stop=(b == 1),
+            )
+
         def down(c, nt, cols, acc):
             for b in range(2):
-                nc.tensor.matmul_mx(
-                    out=acc,
-                    lhsT=wd[:, b, P * nt : P * (nt + 1)].bitcast(FP8X4),
-                    lhsT_scale=wd_plane[:].bitcast(U8)[4 * b :, P * nt : P * (nt + 1)],
-                    rhs=h_codes[(c, b)][:, cols].bitcast(FP8X4),
-                    rhs_scale=h_plane[(c, b)][:, cols],
-                    start=(b == 0),
-                    stop=(b == 1),
-                )
+                down_pass(c, b, nt, cols, acc)
 
         def down_chunk(c, next_stage):
             sums = []
@@ -276,14 +276,26 @@ def tile_list_gmlpt_silu_gate_kernel(
             c0 = CHUNK * LAST + QUARTER * q
             nc.sync.dma_start(out=out[:, c0 : c0 + QUARTER].rearrange("(nt p) j -> p nt j", p=P), in_=res[:])
 
+        def finish_at_the_end():
+            cols = slice(CHUNK - QUARTER, CHUNK)
+            sums = [banks[PACK - 1 + nt][:, :QUARTER] for nt in range(2)]
+            for b in range(2):
+                for nt in range(2):
+                    down_pass(LAST, b, nt, cols, sums[nt])
+            for nt, queue in enumerate((nc.scalar, nc.sync)):
+                res = held([P, QUARTER], F32, "res_end%d" % nt)
+                nc.vector.tensor_tensor(out=res[:], in0=sums[nt], in1=last_gates[:, nt, cols], op=MULT)
+                queue.dma_start(out=out[P * nt : P * (nt + 1), J - QUARTER :], in_=res[:])
+
         gather_plane()
-        gather_words(0, 0)
+        gather_words(0, 0, 2)
+        gather_words(2, 0)
         for a in range(2):
             for pair in range(2):
                 cast_wg(0, a, staging[a], pair)
-        quantise_wg(0, 0, staging[0], 0, PASS)
-        gather_words(1, 0, 2, tag="wg_raw00")
         permute_wu_plane()
+        quantise_wg(0, 0, staging[0], 0, PASS)
+        gather_words(LAST, 0, tag="wg_raw00")
         for c in range(2):
             for t in range(PACK):
                 gate_pass(c, 0, t, 0, banks[PACK * c + t])
@@ -334,7 +346,7 @@ def tile_list_gmlpt_silu_gate_kernel(
 
         for done, (c, b) in enumerate(((1, 1), (2, 1), (LAST, 0))):
             act = gate_part(c, b, 0, (0, 1))
-            stage = staging[(done + 3) % 4]
+            stage = staging[done - 1]
             for q in range(PACK):
                 up_sums(c, b, q, banks[UP + q])
                 if q == 0:
@@ -344,7 +356,6 @@ def tile_list_gmlpt_silu_gate_kernel(
                 if q == PACK - 2:
                     sums = down_chunk(done, staging[done])
                     if done == 0:
-                        gather_words(LAST, 0, tag="wg_raw10")
                         gather_words(LAST, 1, tag="wu_raw1")
             gate_and_store(done, 0, sums[0])
             quantise_h(c, b, stage, 0, CHUNK)
@@ -358,19 +369,4 @@ def tile_list_gmlpt_silu_gate_kernel(
                 quantise_h(LAST, 1, staging[2], QUARTER * (q - 1), QUARTER * q)
         for q in range(PACK - 1):
             finish_last_quarter(q)
-        cols = slice(CHUNK - QUARTER, CHUNK)
-        for b in range(2):
-            for nt in range(2):
-                nc.tensor.matmul_mx(
-                    out=banks[PACK - 1 + nt][:, :QUARTER],
-                    lhsT=wd[:, b, P * nt : P * (nt + 1)].bitcast(FP8X4),
-                    lhsT_scale=wd_plane[:].bitcast(U8)[4 * b :, P * nt : P * (nt + 1)],
-                    rhs=h_codes[(LAST, b)][:, cols].bitcast(FP8X4),
-                    rhs_scale=h_plane[(LAST, b)][:, cols],
-                    start=(b == 0),
-                    stop=(b == 1),
-                )
-        for nt, queue in enumerate((nc.scalar, nc.sync)):
-            res = held([P, QUARTER], F32, "res_end%d" % nt)
-            nc.vector.tensor_tensor(out=res[:], in0=banks[PACK - 1 + nt][:, :QUARTER], in1=last_gates[:, nt, cols], op=MULT)
-            queue.dma_start(out=out[P * nt : P * (nt + 1), J - QUARTER :], in_=res[:])
+        finish_at_the_end()

@@ -24,8 +24,6 @@ LAST = CHUNKS - 1
 QUARTER = CHUNK // PACK
 LIST_COLS = CHUNK // 16
 UP = 4
-STEPPED_ROWS = 13
-STEPPED_END = 8 * STEPPED_ROWS
 
 
 def tile_list_gmlpt_silu_gate_kernel(
@@ -72,18 +70,28 @@ def tile_list_gmlpt_silu_gate_kernel(
 
         gate = [held([P, T], F32, "gate%d" % nt) for nt in range(2)]
 
-        tab_plane = held([P, T // 4], I32, "tab_plane")
+        tab_rows = held([P, T // 4], I32, "tab_rows")
         nc.sync.dma_start(offsets[:], offs)
-        for lo, hi in ((STEPPED_END, P - 16), (P - 16, P)):
-            nc.sync.dma_start(
-                out=tab_plane[lo:hi, :], in_=tab_scales.rearrange("a q t -> (a q) t")[: hi - lo, :].bitcast(I32)
-            )
-        for r in range(4):
-            queue = nc.scalar if r < 2 else nc.sync
-            queue.dma_start(
-                out=tab_plane[r:STEPPED_END:4, :],
-                in_=tab_scales[:, r : r + STEPPED_ROWS, :].rearrange("a u t -> u a t").bitcast(I32),
-            )
+        nc.sync.dma_start(out=tab_rows[:32, :], in_=tab_scales.rearrange("a q t -> q a t").bitcast(I32))
+        nc.gpsimd.memset(tab_rows[32:64, :], 0)
+        nc.vector.memset(tab_rows[64:, :], 0)
+
+        def chunk_list(c, count=1):
+            return offsets[:, LIST_COLS * c : LIST_COLS * (c + count)]
+
+        picked_rows = held([P, J], U8, "picked_rows")
+        picked_plane = [held([P, J // 8], I32, "picked_plane%d" % half) for half in range(2)]
+        planes = [picked_plane[c // 2][:].bitcast(U8)[:, CHUNK * (c % 2) : CHUNK * (c % 2 + 1)] for c in range(CHUNKS)]
+
+        def gather_plane():
+            nc.vector.tensor_copy(out=picked_rows[:], in_=tab_rows[:].bitcast(U8).indirect(chunk_list(0, CHUNKS)))
+
+        def move_plane(half):
+            cols = slice(J // 8 * half, J // 8 * (half + 1))
+            for r in range(4):
+                nc.sync.dma_start(
+                    out=picked_plane[half][r::4, :], in_=picked_rows[:].bitcast(I32)[2 * r : 2 * r + 32, cols]
+                )
 
         warm = held([P, 16], F32, "warm")
         warm_out = held([P, 16], F32, "warm_out")
@@ -92,11 +100,14 @@ def tile_list_gmlpt_silu_gate_kernel(
 
         load_tab(0)
         load_wg(0, 0)
-        wu_plane_raw = load_scales(wu_scales, R, "wu_plane_raw")
         load_wg(0, 1)
+        gather_plane()
+        move_plane(0)
         load_tab(1)
+        wu_plane_raw = load_scales(wu_scales, R, "wu_plane_raw")
         load_wu(0)
         load_wu(1)
+        move_plane(1)
         load_wg(1, 0)
         load_wg(1, 1)
         for nt in range(2):
@@ -105,9 +116,6 @@ def tile_list_gmlpt_silu_gate_kernel(
         wd = held([P, 2, N], I32, "wd")
         nc.sync.dma_start(out=wd[:], in_=wd_words.rearrange("a p n i -> p a (n i)").bitcast(I32))
 
-        def chunk_list(c, count=1):
-            return offsets[:, LIST_COLS * c : LIST_COLS * (c + count)]
-
         words = {}
 
         def gather_words(c, a, count=1, tag=""):
@@ -115,12 +123,6 @@ def tile_list_gmlpt_silu_gate_kernel(
             nc.vector.tensor_copy(out=picked_words[:], in_=tab[a][:].bitcast(U32).indirect(chunk_list(c, count)))
             for i in range(count):
                 words[(c + i, a)] = picked_words[:, CHUNK * i : CHUNK * (i + 1)]
-
-        picked_plane = held([P, J], U8, "picked_plane")
-        planes = [picked_plane[:, CHUNK * c : CHUNK * (c + 1)] for c in range(CHUNKS)]
-
-        def gather_plane():
-            nc.vector.tensor_copy(out=picked_plane[:], in_=tab_plane[:].bitcast(U8).indirect(chunk_list(0, CHUNKS)))
 
         wu = {}
 
@@ -287,13 +289,11 @@ def tile_list_gmlpt_silu_gate_kernel(
                 nc.vector.tensor_tensor(out=res[:], in0=sums[nt], in1=last_gates[:, nt, cols], op=MULT)
                 queue.dma_start(out=out[P * nt : P * (nt + 1), J - QUARTER :], in_=res[:])
 
-        gather_plane()
         gather_words(0, 0, 2)
         gather_words(2, 0)
         for a in range(2):
             for pair in range(2):
                 cast_wg(0, a, staging[a], pair)
-        permute_wu_plane()
         quantise_wg(0, 0, staging[0], 0, PASS)
         gather_words(LAST, 0, tag="wg_raw00")
         for c in range(2):
@@ -305,6 +305,7 @@ def tile_list_gmlpt_silu_gate_kernel(
         act_first = gate_part(0, 0, 0, (1,))
         gather_words(1, 1)
         act = gate_part(1, 0, UP, (1,))
+        permute_wu_plane()
         permute_wu(0)
         gather_words(2, 1, tag="wu_raw0")
         up_part(0, 0, act_first, 0, staging[2])

@@ -62,7 +62,7 @@ def tile_list_gmlpt_silu_gate_kernel(
             rows = wu_words.rearrange("a p r i -> p a (r i)")
             nc.sync.dma_start(out=wu_raw[b][:], in_=rows[:, :, 4 * PASS * b : 4 * PASS * (b + 1)].bitcast(I32))
 
-        wg_raw = {(b, a): held([P, PACK, PASS], F32, "wg_raw%d%d" % (b, a)) for b in range(2) for a in range(2)}
+        wg_raw = {(b, a): held([P, PACK, PASS], F32, "wg_raw%d%d" % (b, a)) for b, a in ((0, 0), (1, 0), (1, 1))}
 
         def load_wg(b, a):
             rows = wg[PASS * a : PASS * (a + 1), PASS * b : PASS * (b + 1)].rearrange("(p j) c -> p j c", j=PACK)
@@ -79,18 +79,18 @@ def tile_list_gmlpt_silu_gate_kernel(
         def chunk_list(c, count=1):
             return offsets[:, LIST_COLS * c : LIST_COLS * (c + count)]
 
-        picked_rows = held([P, J], U8, "picked_rows")
+        picked_rows = [held([P, J // 2], U8, "picked_rows%d" % half) for half in range(2)]
         picked_plane = [held([P, J // 8], I32, "picked_plane%d" % half) for half in range(2)]
         planes = [picked_plane[c // 2][:].bitcast(U8)[:, CHUNK * (c % 2) : CHUNK * (c % 2 + 1)] for c in range(CHUNKS)]
 
-        def gather_plane():
-            nc.vector.tensor_copy(out=picked_rows[:], in_=tab_rows[:].bitcast(U8).indirect(chunk_list(0, CHUNKS)))
+        def gather_plane(half):
+            window = tab_rows[:].bitcast(U8)
+            nc.vector.tensor_copy(out=picked_rows[half][:], in_=window.indirect(chunk_list(2 * half, 2)))
 
         def move_plane(half):
-            cols = slice(J // 8 * half, J // 8 * (half + 1))
             for r in range(4):
                 nc.sync.dma_start(
-                    out=picked_plane[half][r::4, :], in_=picked_rows[:].bitcast(I32)[2 * r : 2 * r + 32, cols]
+                    out=picked_plane[half][r::4, :], in_=picked_rows[half][:].bitcast(I32)[2 * r : 2 * r + 32, :]
                 )
 
         warm = held([P, 16], F32, "warm")
@@ -100,10 +100,14 @@ def tile_list_gmlpt_silu_gate_kernel(
 
         load_tab(0)
         load_wg(0, 0)
-        load_wg(0, 1)
-        gather_plane()
+        for half in range(2):
+            gather_plane(half)
         move_plane(0)
         load_tab(1)
+        second = wg[PASS : 2 * PASS, :PASS].rearrange("(p j) c -> p j c", j=PACK)
+        wg_halves = [held([P, PACK, PASS // 2], F32, "wg_half%d" % half) for half in range(2)]
+        for half in range(2):
+            nc.sync.dma_start(out=wg_halves[half][:], in_=second[:, :, PASS // 2 * half : PASS // 2 * (half + 1)])
         wu_plane_raw = load_scales(wu_scales, R, "wu_plane_raw")
         load_wu(0)
         load_wu(1)
@@ -291,20 +295,27 @@ def tile_list_gmlpt_silu_gate_kernel(
 
         gather_words(0, 0, 2)
         gather_words(2, 0)
-        for a in range(2):
-            for pair in range(2):
-                cast_wg(0, a, staging[a], pair)
+        for pair in range(2):
+            cast_wg(0, 0, staging[0], pair)
         quantise_wg(0, 0, staging[0], 0, PASS)
         gather_words(LAST, 0, tag="wg_raw00")
         for c in range(2):
             for t in range(PACK):
                 gate_pass(c, 0, t, 0, banks[PACK * c + t])
-        quantise_wg(0, 1, staging[1], 0, PASS)
 
-        gather_words(0, 1)
-        act_first = gate_part(0, 0, 0, (1,))
-        gather_words(1, 1)
-        act = gate_part(1, 0, UP, (1,))
+        gather_words(0, 1, 2)
+        second_stage = staging[1][:].rearrange("p (t h m j) -> p h m t j", t=PACK, h=2, j=PACK)
+        halves = [half[:].rearrange("p j (m t) -> p m t j", t=PACK) for half in wg_halves]
+        nc.scalar.copy(out=second_stage[:, 0], in_=halves[0])
+        for pair in range(2):
+            rows = slice(2 * pair, 2 * pair + 2)
+            nc.scalar.copy(out=second_stage[:, 1, :, rows], in_=halves[1][:, :, rows])
+            quantise_wg(0, 1, staging[1], PASS // 2 * pair, PASS // 2 * (pair + 1))
+            for c in range(2):
+                for t in (2 * pair, 2 * pair + 1):
+                    gate_pass(c, 0, t, 1, banks[PACK * c + t])
+        act_first = gate_part(0, 0, 0, ())
+        act = gate_part(1, 0, UP, ())
         permute_wu_plane()
         permute_wu(0)
         gather_words(2, 1, tag="wu_raw0")

@@ -152,9 +152,9 @@ def tile_list_gmlpt_silu_gate_kernel(
         wg_plane = {(b, a): held([P, PASS], U8, "wg_plane%d%d" % (b, a)) for b in range(2) for a in range(2)}
 
         def cast_wg(b, a, stage, pair):
-            src = wg_raw[(b, a)][:].rearrange("p j (m t) -> p m t j", t=PACK)
-            dst = stage[:].rearrange("p (t m j) -> p m t j", t=PACK, j=PACK)
-            nc.scalar.copy(out=dst[:, :, 2 * pair : 2 * pair + 2], in_=src[:, :, 2 * pair : 2 * pair + 2])
+            src = wg_raw[(b, a)][:].rearrange("p j (m t) -> p m j t", t=PACK)
+            dst = stage[:].rearrange("p (t m j) -> p m j t", t=PACK, j=PACK)
+            nc.scalar.copy(out=dst[:, :, :, 2 * pair : 2 * pair + 2], in_=src[:, :, :, 2 * pair : 2 * pair + 2])
 
         def quantise_wg(b, a, stage, lo, hi):
             nc.vector.quantize_mx(
@@ -304,12 +304,14 @@ def tile_list_gmlpt_silu_gate_kernel(
                 gate_pass(c, 0, t, 0, banks[PACK * c + t])
 
         gather_words(0, 1, 2)
-        second_stage = staging[1][:].rearrange("p (t h m j) -> p h m t j", t=PACK, h=2, j=PACK)
-        halves = [half[:].rearrange("p j (m t) -> p m t j", t=PACK) for half in wg_halves]
-        nc.scalar.copy(out=second_stage[:, 0], in_=halves[0])
+        second_stage = staging[1][:].rearrange("p (t h m j) -> p h m j t", t=PACK, h=2, j=PACK)
+        halves = [half[:].rearrange("p j (m t) -> p m j t", t=PACK) for half in wg_halves]
         for pair in range(2):
             rows = slice(2 * pair, 2 * pair + 2)
-            nc.scalar.copy(out=second_stage[:, 1, :, rows], in_=halves[1][:, :, rows])
+            nc.scalar.copy(out=second_stage[:, 0, :, :, rows], in_=halves[0][:, :, :, rows])
+        for pair in range(2):
+            rows = slice(2 * pair, 2 * pair + 2)
+            nc.scalar.copy(out=second_stage[:, 1, :, :, rows], in_=halves[1][:, :, :, rows])
             quantise_wg(0, 1, staging[1], PASS // 2 * pair, PASS // 2 * (pair + 1))
             for c in range(2):
                 for t in (2 * pair, 2 * pair + 1):

@@ -105,9 +105,10 @@ def tile_list_gmlpt_silu_gate_kernel(
         move_plane(0)
         load_tab(1)
         second = wg[PASS : 2 * PASS, :PASS].rearrange("(p j) c -> p j c", j=PACK)
-        wg_halves = [held([P, PACK, PASS // 2], F32, "wg_half%d" % half) for half in range(2)]
-        for half in range(2):
-            nc.sync.dma_start(out=wg_halves[half][:], in_=second[:, :, PASS // 2 * half : PASS // 2 * (half + 1)])
+        cuts = (0, PASS // 2, 3 * PASS // 4, PASS)
+        wg_parts = [held([P, PACK, cuts[i + 1] - cuts[i]], F32, "wg_part%d" % i) for i in range(3)]
+        for i in range(3):
+            nc.sync.dma_start(out=wg_parts[i][:], in_=second[:, :, cuts[i] : cuts[i + 1]])
         wu_plane_raw = load_scales(wu_scales, R, "wu_plane_raw")
         load_wu(0)
         load_wu(1)
@@ -304,14 +305,16 @@ def tile_list_gmlpt_silu_gate_kernel(
                 gate_pass(c, 0, t, 0, banks[PACK * c + t])
 
         gather_words(0, 1, 2)
-        second_stage = staging[1][:].rearrange("p (t h m j) -> p h m j t", t=PACK, h=2, j=PACK)
-        halves = [half[:].rearrange("p j (m t) -> p m j t", t=PACK) for half in wg_halves]
+        second_stage = staging[1][:].rearrange("p (t m j) -> p m j t", t=PACK, j=PACK)
+        parts = [part[:].rearrange("p j (m t) -> p m j t", t=PACK) for part in wg_parts]
         for pair in range(2):
             rows = slice(2 * pair, 2 * pair + 2)
-            nc.scalar.copy(out=second_stage[:, 0, :, :, rows], in_=halves[0][:, :, :, rows])
-        for pair in range(2):
-            rows = slice(2 * pair, 2 * pair + 2)
-            nc.scalar.copy(out=second_stage[:, 1, :, :, rows], in_=halves[1][:, :, :, rows])
+            for i in range(3):
+                dst = second_stage[:, cuts[i] // PACK : cuts[i + 1] // PACK, :, rows]
+                if i == 1:
+                    nc.vector.tensor_copy(out=dst, in_=parts[i][:, :, :, rows])
+                else:
+                    nc.scalar.copy(out=dst, in_=parts[i][:, :, :, rows])
             quantise_wg(0, 1, staging[1], PASS // 2 * pair, PASS // 2 * (pair + 1))
             for c in range(2):
                 for t in (2 * pair, 2 * pair + 1):

@@ -46,9 +46,9 @@ def tile_list_gmlpt_silu_gate_kernel(
         def load_tab(a):
             nc.sync.dma_start(out=tab[a][:], in_=tab_words[a].rearrange("p t i -> p (t i)").bitcast(I32))
 
-        def load_scales(dram, width, name):
+        def load_scales(dram, width, name, engine):
             plane = held([P, width // 4], I32, name)
-            nc.vector.memset(plane[:], 0)
+            engine.memset(plane[:], 0)
             for quad in range(4):
                 nc.sync.dma_start(
                     out=plane[32 * quad : 32 * quad + 8, :],
@@ -56,23 +56,19 @@ def tile_list_gmlpt_silu_gate_kernel(
                 )
             return plane
 
-        wu_raw = [held([P, 2, PASS], I32, "wu_raw%d" % b) for b in range(2)]
-
-        def load_wu(b):
-            rows = wu_words.rearrange("a p r i -> p a (r i)")
-            nc.sync.dma_start(out=wu_raw[b][:], in_=rows[:, :, 4 * PASS * b : 4 * PASS * (b + 1)].bitcast(I32))
-
-        wg_raw = {(b, a): held([P, PACK, PASS], F32, "wg_raw%d%d" % (b, a)) for b, a in ((0, 0), (1, 0), (1, 1))}
+        wu_rows = wu_words.rearrange("a p r i -> p a (r i)")
+        wu_first = [held([P, PASS], I32, "wu_first%d" % a) for a in range(2)]
+        wu_second = held([P, 2, PASS], I32, "wu_second")
+        wg_raw = {(b, a): held([P, PACK, PASS], F32, "wg_raw%d%d" % (b, a)) for b in range(2) for a in range(2)}
 
         def load_wg(b, a):
             rows = wg[PASS * a : PASS * (a + 1), PASS * b : PASS * (b + 1)].rearrange("(p j) c -> p j c", j=PACK)
             nc.sync.dma_start(out=wg_raw[(b, a)][:], in_=rows)
 
-        gate = [held([P, T], F32, "gate%d" % nt) for nt in range(2)]
-
         tab_rows = held([P, T // 4], I32, "tab_rows")
         nc.sync.dma_start(offsets[:], offs)
         nc.sync.dma_start(out=tab_rows[:32, :], in_=tab_scales.rearrange("a q t -> q a t").bitcast(I32))
+        wu_plane_raw = load_scales(wu_scales, R, "wu_plane_raw", nc.gpsimd)
         nc.gpsimd.memset(tab_rows[32:64, :], 0)
         nc.vector.memset(tab_rows[64:, :], 0)
 
@@ -98,46 +94,6 @@ def tile_list_gmlpt_silu_gate_kernel(
         nc.vector.memset(warm[:], 0.0)
         nc.scalar.activation(out=warm_out[:], in_=warm[:], func=SILU)
 
-        load_tab(0)
-        load_wg(0, 0)
-        for half in range(2):
-            gather_plane(half)
-        move_plane(0)
-        load_tab(1)
-        second = wg[PASS : 2 * PASS, :PASS].rearrange("(p j) c -> p j c", j=PACK)
-        cuts = (0, PASS // 2, 3 * PASS // 4, PASS)
-        wg_parts = [held([P, PACK, cuts[i + 1] - cuts[i]], F32, "wg_part%d" % i) for i in range(3)]
-        for i in range(3):
-            nc.sync.dma_start(out=wg_parts[i][:], in_=second[:, :, cuts[i] : cuts[i + 1]])
-        wu_plane_raw = load_scales(wu_scales, R, "wu_plane_raw")
-        load_wu(0)
-        load_wu(1)
-        move_plane(1)
-        load_wg(1, 0)
-        load_wg(1, 1)
-        for nt in range(2):
-            nc.sync.dma_start(out=gate[nt][:], in_=gT[P * nt : P * (nt + 1), :])
-        wd_plane = load_scales(wd_scales, N, "wd_plane")
-        wd = held([P, 2, N], I32, "wd")
-        nc.sync.dma_start(out=wd[:], in_=wd_words.rearrange("a p n i -> p a (n i)").bitcast(I32))
-
-        words = {}
-
-        def gather_words(c, a, count=1, tag=""):
-            picked_words = keep.tile([P, CHUNK * count], U32, name="words%d%d" % (c, a), tag=tag, align_bytes=64)
-            nc.vector.tensor_copy(out=picked_words[:], in_=tab[a][:].bitcast(U32).indirect(chunk_list(c, count)))
-            for i in range(count):
-                words[(c + i, a)] = picked_words[:, CHUNK * i : CHUNK * (i + 1)]
-
-        wu = {}
-
-        def permute_wu(b):
-            wu[b] = held([P, PACK, 2, P], I32, "wu%d" % b)
-            nc.vector.tensor_copy(
-                out=wu[b][:].rearrange("p t a (c i) -> p (a c) t i", i=4),
-                in_=wu_raw[b][:].rearrange("p a (c i t) -> p (a c) t i", i=4, t=PACK),
-            )
-
         wu_plane = held([P, PACK, 2, P], U8, "wu_plane")
 
         def permute_wu_plane():
@@ -146,22 +102,71 @@ def tile_list_gmlpt_silu_gate_kernel(
                 in_=wu_plane_raw[:].bitcast(U8).rearrange("p (c i t) -> p c t i", i=16, t=PACK),
             )
 
+        permute_wu_plane()
+        load_tab(0)
+        nc.sync.dma_start(out=wu_first[0][:], in_=wu_rows[:, 0, : 4 * PASS].bitcast(I32))
+        for half in range(2):
+            gather_plane(half)
+        move_plane(0)
+        load_tab(1)
+        nc.sync.dma_start(out=wu_first[1][:], in_=wu_rows[:, 1, : 4 * PASS].bitcast(I32))
+        move_plane(1)
+        load_wg(0, 0)
+        load_wg(0, 1)
+        nc.sync.dma_start(out=wu_second[:], in_=wu_rows[:, :, 4 * PASS :].bitcast(I32))
+        load_wg(1, 0)
+        load_wg(1, 1)
+        gate = [held([P, T], F32, "gate0")]
+        nc.sync.dma_start(out=gate[0][:], in_=gT[:P, :])
+        wd_plane = load_scales(wd_scales, N, "wd_plane", nc.vector)
+        wd = held([P, 2, N], I32, "wd")
+        nc.sync.dma_start(out=wd[:], in_=wd_words.rearrange("a p n i -> p a (n i)").bitcast(I32))
+
+        words = {}
+
+        def gather_words(c, a, tag=""):
+            picked_words = keep.tile([P, CHUNK], U32, name="words%d%d" % (c, a), tag=tag, align_bytes=64)
+            nc.vector.tensor_copy(out=picked_words[:], in_=tab[a][:].bitcast(U32).indirect(chunk_list(c)))
+            words[(c, a)] = picked_words
+
+        wu = {}
+
+        def permute_wu_first(a):
+            ordered = held([P, PACK, P], I32, "wu0%d" % a)
+            nc.scalar.copy(
+                out=ordered[:].bitcast(U32).rearrange("p t m -> p m t"),
+                in_=wu_first[a][:].bitcast(U32).rearrange("p (m t) -> p m t", t=PACK),
+            )
+            wu[(0, a)] = ordered
+
+        def permute_wu_second():
+            ordered = keep.tile([P, 2, PACK, P], I32, name="wu1", tag="wg_raw01", align_bytes=64)
+            nc.vector.tensor_copy(
+                out=ordered[:].rearrange("p a t (c i) -> p a c t i", i=4),
+                in_=wu_second[:].rearrange("p a (c i t) -> p a c t i", i=4, t=PACK),
+            )
+            for a in range(2):
+                wu[(1, a)] = ordered[:, a]
+
         staging = [held([P, PACK * PASS], BF16, "staging%d" % i) for i in range(4)]
-        late_tile = keep.tile([P, 2, PACK * PASS], BF16, name="late_stage", tag="wu_raw1", align_bytes=64)
-        late_stage = [late_tile[:, a, :] for a in range(2)]
         wg_codes = {(b, a): held([P, PASS], U32, "wg_codes%d%d" % (b, a)) for b in range(2) for a in range(2)}
         wg_plane = {(b, a): held([P, PASS], U8, "wg_plane%d%d" % (b, a)) for b in range(2) for a in range(2)}
 
-        def cast_wg(b, a, stage, pair):
-            src = wg_raw[(b, a)][:].rearrange("p j (m t) -> p m j t", t=PACK)
-            dst = stage[:].rearrange("p (t m j) -> p m j t", t=PACK, j=PACK)
-            nc.scalar.copy(out=dst[:, :, :, 2 * pair : 2 * pair + 2], in_=src[:, :, :, 2 * pair : 2 * pair + 2])
+        long_stage = held([P, 3 * PACK * PASS // 2], BF16, "long_stage")
+        h_stage = long_stage[:, : PACK * PASS]
+        next_stage = long_stage[:, PACK * PASS // 2 :]
+        wg_stage = {(0, 0): staging[0][:], (0, 1): staging[1][:], (1, 0): next_stage, (1, 1): staging[3][:]}
 
-        def quantise_wg(b, a, stage, lo, hi):
+        def cast_wg(b, a, pair, copy):
+            src = wg_raw[(b, a)][:].rearrange("p j (m t) -> p m j t", t=PACK)
+            dst = wg_stage[(b, a)].rearrange("p (t m j) -> p m j t", t=PACK, j=PACK)
+            copy(out=dst[:, :, :, 2 * pair : 2 * pair + 2], in_=src[:, :, :, 2 * pair : 2 * pair + 2])
+
+        def quantise_wg(b, a, lo, hi):
             nc.vector.quantize_mx(
                 out=wg_codes[(b, a)][:, lo:hi].bitcast(FP8X4),
                 scales=wg_plane[(b, a)][:, lo:hi],
-                in_=stage[:, PACK * lo : PACK * hi],
+                in_=wg_stage[(b, a)][:, PACK * lo : PACK * hi],
             )
 
         h_codes = {(c, b): held([P, CHUNK], U32, "h_codes%d%d" % (c, b)) for c in range(CHUNKS) for b in range(2)}
@@ -178,56 +183,53 @@ def tile_list_gmlpt_silu_gate_kernel(
                 stop=(a == 1),
             )
 
-        def gate_rows(c, b, t, act, bank, passes):
-            for a in passes:
-                gate_pass(c, b, t, a, bank)
-            nc.scalar.activation(out=act[:, t, :], in_=bank[:], func=SILU)
-
-        def gate_part(c, b, first_bank, passes):
+        def gate_part(c, b, first_bank, by_pass=False):
             act = ring.tile([P, PACK, CHUNK], F32, name="act")
+            if by_pass:
+                for t in range(PACK):
+                    gate_pass(c, b, t, 0, banks[first_bank + t])
             for t in range(PACK):
-                gate_rows(c, b, t, act, banks[first_bank + t], passes)
+                for a in range(1 if by_pass else 0, 2):
+                    gate_pass(c, b, t, a, banks[first_bank + t])
+                nc.scalar.activation(out=act[:, t, :], in_=banks[first_bank + t][:], func=SILU)
             return act
+
+        def up_pass(c, b, t, a, cols, acc):
+            nc.tensor.matmul_mx(
+                out=acc,
+                lhsT=wu[(b, a)][:, t, :].bitcast(FP8X4),
+                lhsT_scale=wu_plane[4 * a :, t, b, :],
+                rhs=words[(c, a)][:, cols].bitcast(FP8X4),
+                rhs_scale=planes[c][4 * a :, cols],
+                start=(a == 0),
+                stop=(a == 1),
+            )
 
         def up_view(bank):
             return bank[:].rearrange("p (t n) -> p t n", t=PACK)
 
+        def quarter(q):
+            return slice(QUARTER * q, QUARTER * (q + 1))
+
         def up_sums(c, b, q, bank):
-            cols = slice(QUARTER * q, QUARTER * (q + 1))
             for t in range(PACK):
                 for a in range(2):
-                    nc.tensor.matmul_mx(
-                        out=up_view(bank)[:, t, :],
-                        lhsT=wu[b][:, t, a, :].bitcast(FP8X4),
-                        lhsT_scale=wu_plane[4 * a :, t, b, :],
-                        rhs=words[(c, a)][:, cols].bitcast(FP8X4),
-                        rhs_scale=planes[c][4 * a :, cols],
-                        start=(a == 0),
-                        stop=(a == 1),
-                    )
+                    up_pass(c, b, t, a, quarter(q), up_view(bank)[:, t, :])
 
-        def multiply(q, act, up, stage, engine=nc.vector):
+        def multiply(q, act, up, stage, engine=nc.vector, count=1):
             engine.tensor_tensor(
-                out=stage[:, PASS * q : PASS * (q + 1)].rearrange("p (n i t) -> p n t i", i=2, t=PACK),
-                in0=up_view(up).rearrange("p t (n i) -> p n t i", i=2),
-                in1=act[:, :, QUARTER * q : QUARTER * (q + 1)].rearrange("p t (n i) -> p n t i", i=2),
+                out=stage[:, PASS * q : PASS * (q + count)].rearrange("p (n i t) -> p n t i", i=2, t=PACK),
+                in0=up.rearrange("p t (n i) -> p n t i", i=2),
+                in1=act[:, :, QUARTER * q : QUARTER * (q + count)].rearrange("p t (n i) -> p n t i", i=2),
                 op=MULT,
             )
-
-        def up_quarter(c, b, q, act, bank, stage):
-            up_sums(c, b, q, bank)
-            multiply(q, act, bank, stage)
 
         def share_first_quarter(act, stage):
             parked = ring.tile([P, CHUNK], F32, name="parked")
             nc.scalar.copy(out=parked[:], in_=banks[UP][:])
-            multiply(0, act, parked, stage, nc.gpsimd)
+            multiply(0, act, up_view(parked), stage, nc.gpsimd)
 
-        def up_part(c, b, act, first_bank, stage):
-            for q in range(PACK):
-                up_quarter(c, b, q, act, banks[first_bank + q], stage)
-
-        def quantise_h(c, b, stage, lo, hi):
+        def quantise_h(c, b, stage, lo=0, hi=CHUNK):
             nc.vector.quantize_mx(
                 out=h_codes[(c, b)][:, lo:hi].bitcast(FP8X4),
                 scales=h_plane[(c, b)][:, lo:hi],
@@ -266,7 +268,6 @@ def tile_list_gmlpt_silu_gate_kernel(
             nc.vector.tensor_tensor(out=res[:], in0=gate[nt][:].indirect(chunk_list(c)), in1=y[:], op=MULT)
             nc.sync.dma_start(out=out[P * nt : P * (nt + 1), CHUNK * c : CHUNK * (c + 1)], in_=res[:])
 
-        last_gates = wg_raw[(1, 1)][:, 0:2, :]
 
         def pick_last_gates(nt):
             nc.vector.tensor_copy(out=last_gates[:, nt, :], in_=gate[nt][:].indirect(chunk_list(LAST)))
@@ -294,96 +295,90 @@ def tile_list_gmlpt_silu_gate_kernel(
                 nc.vector.tensor_tensor(out=res[:], in0=sums[nt], in1=last_gates[:, nt, cols], op=MULT)
                 queue.dma_start(out=out[P * nt : P * (nt + 1), J - QUARTER :], in_=res[:])
 
-        gather_words(0, 0, 2)
+        everything = slice(0, CHUNK)
+        gather_words(0, 0)
+        permute_wu_first(0)
+        gather_words(1, 0)
         gather_words(2, 0)
-        for pair in range(2):
-            cast_wg(0, 0, staging[0], pair)
-        quantise_wg(0, 0, staging[0], 0, PASS)
-        gather_words(LAST, 0, tag="wg_raw00")
+        gather_words(LAST, 0)
         for c in range(2):
             for t in range(PACK):
-                gate_pass(c, 0, t, 0, banks[PACK * c + t])
+                up_pass(c, 0, t, 0, everything, banks[PACK * c + t][:])
 
-        gather_words(0, 1, 2)
-        second_stage = staging[1][:].rearrange("p (t m j) -> p m j t", t=PACK, j=PACK)
-        parts = [part[:].rearrange("p j (m t) -> p m j t", t=PACK) for part in wg_parts]
-        for pair in range(2):
-            rows = slice(2 * pair, 2 * pair + 2)
-            for i in range(3):
-                dst = second_stage[:, cuts[i] // PACK : cuts[i + 1] // PACK, :, rows]
-                if i == 1:
-                    nc.vector.tensor_copy(out=dst, in_=parts[i][:, :, :, rows])
-                else:
-                    nc.scalar.copy(out=dst, in_=parts[i][:, :, :, rows])
-            quantise_wg(0, 1, staging[1], PASS // 2 * pair, PASS // 2 * (pair + 1))
-            for c in range(2):
-                for t in (2 * pair, 2 * pair + 1):
-                    gate_pass(c, 0, t, 1, banks[PACK * c + t])
-        act_first = gate_part(0, 0, 0, ())
-        act = gate_part(1, 0, UP, ())
-        permute_wu_plane()
-        permute_wu(0)
-        gather_words(2, 1, tag="wu_raw0")
-        up_part(0, 0, act_first, 0, staging[2])
-        permute_wu(1)
-        for a in range(2):
-            cast_wg(1, a, late_stage[a], 0)
+        permute_wu_first(1)
+        kept_up = [held([P, PACK, CHUNK], F32, "kept_up%d" % c) for c in range(2)]
+        for c in range(2):
+            gather_words(c, 1)
+            for t in range(PACK):
+                up_pass(c, 0, t, 1, everything, banks[PACK * c + t][:])
+                nc.scalar.copy(out=kept_up[c][:, t, :], in_=banks[PACK * c + t][:])
+        gather_words(2, 1)
         for q in range(PACK):
-            up_quarter(1, 0, q, act, banks[UP + q], staging[3])
-            if q == 0:
-                quantise_h(0, 0, staging[2], 0, CHUNK)
-
-        act = gate_part(2, 0, 0, (0, 1))
-        for a in range(2):
-            cast_wg(1, a, late_stage[a], 1)
-        for a in range(2):
-            quantise_wg(1, a, late_stage[a], 0, PASS // 2)
-        quantise_h(1, 0, staging[3], 0, CHUNK)
-        up_sums(2, 0, 0, banks[UP])
-        share_first_quarter(act, staging[3])
-        for q in range(1, PACK):
-            up_quarter(2, 0, q, act, banks[UP + q], staging[3])
-
-        act = ring.tile([P, PACK, CHUNK], F32, name="act")
+            up_sums(2, 0, q, banks[q])
         for pair in range(2):
-            if pair == 1:
-                for a in range(2):
-                    quantise_wg(1, a, late_stage[a], PASS // 2, PASS)
-            for t in (2 * pair, 2 * pair + 1):
-                gate_rows(0, 1, t, act, banks[t], (0, 1))
-            for q in (2 * pair, 2 * pair + 1):
-                up_sums(0, 1, q, banks[UP + q])
-        pick_last_gates(0)
-        quantise_h(2, 0, staging[3], 0, CHUNK)
-        share_first_quarter(act, staging[3])
-        for q in range(1, PACK):
-            multiply(q, act, banks[UP + q], staging[3])
-        pick_last_gates(1)
-        quantise_h(0, 1, staging[3], 0, CHUNK)
+            cast_wg(0, 0, pair, nc.vector.tensor_copy)
+        quantise_wg(0, 0, 0, PASS)
+        cast_wg(0, 1, 0, nc.vector.tensor_copy)
+        cast_wg(0, 1, 1, nc.scalar.copy)
+        for pair in range(2):
+            quantise_wg(0, 1, PASS // 2 * pair, PASS // 2 * (pair + 1))
+        act_2 = gate_part(2, 0, UP, by_pass=True)
+        permute_wu_second()
+        gate.append(keep.tile([P, T], F32, name="gate1", tag="tab0", align_bytes=64))
+        nc.sync.dma_start(out=gate[1][:], in_=gT[P:, :])
+        act_0 = gate_part(0, 0, UP)
+        for q in range(PACK):
+            multiply(q, act_2, up_view(banks[q]), staging[2])
+        act_1 = gate_part(1, 0, 0)
+        for pair in range(2):
+            cast_wg(1, 0, pair, nc.vector.tensor_copy)
+        quantise_h(2, 0, staging[2])
+        quantise_wg(1, 0, 0, PASS)
+        for pair in range(2):
+            cast_wg(1, 1, pair, nc.scalar.copy)
+        multiply(0, act_0, kept_up[0][:], h_stage, count=4)
+        for q in range(PACK):
+            up_sums(0, 1, q, banks[UP + q])
+        for pair in range(2):
+            quantise_wg(1, 1, PASS // 2 * pair, PASS // 2 * (pair + 1))
+        multiply(2, act_1, kept_up[1][:, :, 2 * QUARTER :], next_stage, count=2)
+        quantise_h(0, 0, h_stage)
+        act = gate_part(0, 1, 0, by_pass=True)
+        gather_words(LAST, 1, tag="staging3")
+        for q in range(2):
+            multiply(q, act_1, kept_up[1][:, :, quarter(q)], next_stage, nc.gpsimd)
+        for q in range(PACK):
+            multiply(q, act, up_view(banks[UP + q]), staging[0])
+        quantise_h(0, 1, staging[0])
+        quantise_h(1, 0, next_stage)
 
+        stages = (next_stage, staging[2], staging[0], staging[2])
         for done, (c, b) in enumerate(((1, 1), (2, 1), (LAST, 0))):
-            act = gate_part(c, b, 0, (0, 1))
-            stage = staging[done - 1]
+            act = gate_part(c, b, 0)
+            stage = stages[done]
             for q in range(PACK):
                 up_sums(c, b, q, banks[UP + q])
                 if q == 0:
                     share_first_quarter(act, stage)
                 else:
-                    multiply(q, act, banks[UP + q], stage)
+                    multiply(q, act, up_view(banks[UP + q]), stage)
                 if q == PACK - 2:
-                    sums = down_chunk(done, staging[done])
-                    if done == 0:
-                        gather_words(LAST, 1, tag="wu_raw1")
+                    sums = down_chunk(done, stages[done + 1])
             gate_and_store(done, 0, sums[0])
-            quantise_h(c, b, stage, 0, CHUNK)
+            quantise_h(c, b, stage)
             gate_and_store(done, 1, sums[1])
+            if done == 1:
+                last_gates = keep.tile([P, 2, CHUNK], F32, name="last_gates", tag="kept_up1", align_bytes=64)
+                for nt in range(2):
+                    pick_last_gates(nt)
 
-        act = gate_part(LAST, 1, 0, (0, 1))
+        act = gate_part(LAST, 1, 0)
         for q in range(PACK + 1):
             if q < PACK:
-                up_quarter(LAST, 1, q, act, banks[UP + q], staging[2])
+                up_sums(LAST, 1, q, banks[UP + q])
+                multiply(q, act, up_view(banks[UP + q]), stages[3])
             if q >= 1:
-                quantise_h(LAST, 1, staging[2], QUARTER * (q - 1), QUARTER * q)
+                quantise_h(LAST, 1, stages[3], QUARTER * (q - 1), QUARTER * q)
         for q in range(PACK - 1):
             finish_last_quarter(q)
         finish_at_the_end()

@@ -268,6 +268,7 @@ def tile_list_gmlpt_silu_gate_kernel(
             nc.vector.tensor_tensor(out=res[:], in0=gate[nt][:].indirect(chunk_list(c)), in1=y[:], op=MULT)
             nc.sync.dma_start(out=out[P * nt : P * (nt + 1), CHUNK * c : CHUNK * (c + 1)], in_=res[:])
 
+        last_gates = wg_raw[(1, 1)][:, 0:2, :]
 
         def pick_last_gates(nt):
             nc.vector.tensor_copy(out=last_gates[:, nt, :], in_=gate[nt][:].indirect(chunk_list(LAST)))
@@ -324,6 +325,7 @@ def tile_list_gmlpt_silu_gate_kernel(
             quantise_wg(0, 1, PASS // 2 * pair, PASS // 2 * (pair + 1))
         act_2 = gate_part(2, 0, UP, by_pass=True)
         permute_wu_second()
+        gather_words(LAST, 1, tag="staging1")
         gate.append(keep.tile([P, T], F32, name="gate1", tag="tab0", align_bytes=64))
         nc.sync.dma_start(out=gate[1][:], in_=gT[P:, :])
         act_0 = gate_part(0, 0, UP)
@@ -344,7 +346,7 @@ def tile_list_gmlpt_silu_gate_kernel(
         multiply(2, act_1, kept_up[1][:, :, 2 * QUARTER :], next_stage, count=2)
         quantise_h(0, 0, h_stage)
         act = gate_part(0, 1, 0, by_pass=True)
-        gather_words(LAST, 1, tag="staging3")
+        pick_last_gates(0)
         for q in range(2):
             multiply(q, act_1, kept_up[1][:, :, quarter(q)], next_stage, nc.gpsimd)
         for q in range(PACK):
@@ -368,9 +370,7 @@ def tile_list_gmlpt_silu_gate_kernel(
             quantise_h(c, b, stage)
             gate_and_store(done, 1, sums[1])
             if done == 1:
-                last_gates = keep.tile([P, 2, CHUNK], F32, name="last_gates", tag="kept_up1", align_bytes=64)
-                for nt in range(2):
-                    pick_last_gates(nt)
+                pick_last_gates(1)
 
         act = gate_part(LAST, 1, 0)
         for q in range(PACK + 1):

from contextlib import ExitStack

import concourse.mybir as mybir

K, R, N, T, J = 1024, 1024, 256, 4096, 2048
FLOPS = 2 * J * (2 * K * R + R * N)

F32 = mybir.dt.float32
BF16 = mybir.dt.bfloat16
I32 = mybir.dt.int32
U32 = mybir.dt.uint32
U16 = mybir.dt.uint16
U8 = mybir.dt.uint8
FP8X4 = mybir.dt.float8_e4m3fn_x4
MULT = mybir.AluOpType.mult
SILU = mybir.ActivationFunctionType.Silu

P = 128
PACK = 4
PASS = P * PACK
CHUNK = 512
CHUNKS = J // CHUNK
LAST = CHUNKS - 1
QUARTER = CHUNK // PACK
LIST_COLS = CHUNK // 16
UP = 4


def tile_list_gmlpt_silu_gate_kernel(
    tc, tab_words, tab_scales, wg, wu_words, wu_scales, wd_words, wd_scales, gT, offs, out
):
    nc = tc.nc
    with ExitStack() as ctx:
        lists = ctx.enter_context(tc.tile_pool(name="lists", bufs=1))
        keep = ctx.enter_context(tc.tile_pool(name="keep", bufs=1))
        ring = ctx.enter_context(tc.tile_pool(name="ring", bufs=3))
        psum = ctx.enter_context(tc.psum_pool(name="psum", bufs=1))
        banks = [psum.tile([P, CHUNK], F32, name="bank%d" % i) for i in range(8)]

        def held(shape, dtype, name):
            return keep.tile(shape, dtype, name=name, align_bytes=64)

        offsets = lists.tile([P, J // 16], U16, name="offsets")
        tab = [held([P, T], I32, "tab%d" % a) for a in range(2)]

        def load_tab(a):
            nc.sync.dma_start(out=tab[a][:], in_=tab_words[a].rearrange("p t i -> p (t i)").bitcast(I32))

        def load_scales(dram, width, name, engine):
            plane = held([P, width // 4], I32, name)
            engine.memset(plane[:], 0)
            for quad in range(4):
                nc.sync.dma_start(
                    out=plane[32 * quad : 32 * quad + 8, :],
                    in_=dram[:, 4 * quad : 4 * quad + 4, :].bitcast(I32),
                )
            return plane

        wu_rows = wu_words.rearrange("a p r i -> p a (r i)")
        wu_first = [held([P, PASS], I32, "wu_first%d" % a) for a in range(2)]
        wu_second = held([P, 2, PASS], I32, "wu_second")
        wg_raw = {(b, a): held([P, PACK, PASS], F32, "wg_raw%d%d" % (b, a)) for b in range(2) for a in range(2)}

        def load_wg(b, a):
            rows = wg[PASS * a : PASS * (a + 1), PASS * b : PASS * (b + 1)].rearrange("(p j) c -> p j c", j=PACK)
            nc.sync.dma_start(out=wg_raw[(b, a)][:], in_=rows)

        tab_rows = held([P, T // 4], I32, "tab_rows")
        nc.sync.dma_start(offsets[:], offs)
        nc.sync.dma_start(out=tab_rows[:32, :], in_=tab_scales.rearrange("a q t -> q a t").bitcast(I32))
        wu_plane_raw = load_scales(wu_scales, R, "wu_plane_raw", nc.gpsimd)
        nc.gpsimd.memset(tab_rows[32:64, :], 0)
        nc.vector.memset(tab_rows[64:, :], 0)

        def chunk_list(c, count=1):
            return offsets[:, LIST_COLS * c : LIST_COLS * (c + count)]

        picked_rows = [held([P, J // 2], U8, "picked_rows%d" % half) for half in range(2)]
        picked_plane = [held([P, J // 8], I32, "picked_plane%d" % half) for half in range(2)]
        planes = [picked_plane[c // 2][:].bitcast(U8)[:, CHUNK * (c % 2) : CHUNK * (c % 2 + 1)] for c in range(CHUNKS)]

        def gather_plane(half):
            window = tab_rows[:].bitcast(U8)
            nc.vector.tensor_copy(out=picked_rows[half][:], in_=window.indirect(chunk_list(2 * half, 2)))

        def move_plane(half):
            for r in range(4):
                nc.sync.dma_start(
                    out=picked_plane[half][r::4, :], in_=picked_rows[half][:].bitcast(I32)[2 * r : 2 * r + 32, :]
                )

        warm = held([P, 16], F32, "warm")
        warm_out = held([P, 16], F32, "warm_out")
        nc.vector.memset(warm[:], 0.0)
        nc.scalar.activation(out=warm_out[:], in_=warm[:], func=SILU)

        wu_plane = held([P, PACK, 2, P], U8, "wu_plane")

        def permute_wu_plane():
            nc.vector.tensor_copy(
                out=wu_plane[:].rearrange("p t b (c i) -> p (b c) t i", i=16),
                in_=wu_plane_raw[:].bitcast(U8).rearrange("p (c i t) -> p c t i", i=16, t=PACK),
            )

        permute_wu_plane()
        load_tab(0)
        nc.sync.dma_start(out=wu_first[0][:], in_=wu_rows[:, 0, : 4 * PASS].bitcast(I32))
        for half in range(2):
            gather_plane(half)
        move_plane(0)
        load_tab(1)
        nc.sync.dma_start(out=wu_first[1][:], in_=wu_rows[:, 1, : 4 * PASS].bitcast(I32))
        move_plane(1)
        load_wg(0, 0)
        load_wg(0, 1)
        nc.sync.dma_start(out=wu_second[:], in_=wu_rows[:, :, 4 * PASS :].bitcast(I32))
        load_wg(1, 0)
        load_wg(1, 1)
        gate = [held([P, T], F32, "gate0")]
        nc.sync.dma_start(out=gate[0][:], in_=gT[:P, :])
        wd_plane = load_scales(wd_scales, N, "wd_plane", nc.vector)
        wd = held([P, 2, N], I32, "wd")
        nc.sync.dma_start(out=wd[:], in_=wd_words.rearrange("a p n i -> p a (n i)").bitcast(I32))

        words = {}

        def gather_words(c, a, tag=""):
            picked_words = keep.tile([P, CHUNK], U32, name="words%d%d" % (c, a), tag=tag, align_bytes=64)
            nc.vector.tensor_copy(out=picked_words[:], in_=tab[a][:].bitcast(U32).indirect(chunk_list(c)))
            words[(c, a)] = picked_words

        wu = {}

        def permute_wu_first(a):
            ordered = held([P, PACK, P], I32, "wu0%d" % a)
            nc.scalar.copy(
                out=ordered[:].bitcast(U32).rearrange("p t m -> p m t"),
                in_=wu_first[a][:].bitcast(U32).rearrange("p (m t) -> p m t", t=PACK),
            )
            wu[(0, a)] = ordered

        def permute_wu_second():
            ordered = keep.tile([P, 2, PACK, P], I32, name="wu1", tag="wg_raw01", align_bytes=64)
            nc.vector.tensor_copy(
                out=ordered[:].rearrange("p a t (c i) -> p a c t i", i=4),
                in_=wu_second[:].rearrange("p a (c i t) -> p a c t i", i=4, t=PACK),
            )
            for a in range(2):
                wu[(1, a)] = ordered[:, a]

        staging = [held([P, PACK * PASS], BF16, "staging%d" % i) for i in range(4)]
        wg_codes = {(b, a): held([P, PASS], U32, "wg_codes%d%d" % (b, a)) for b in range(2) for a in range(2)}
        wg_plane = {(b, a): held([P, PASS], U8, "wg_plane%d%d" % (b, a)) for b in range(2) for a in range(2)}

        long_stage = held([P, 3 * PACK * PASS // 2], BF16, "long_stage")
        h_stage = long_stage[:, : PACK * PASS]
        next_stage = long_stage[:, PACK * PASS // 2 :]
        wg_stage = {(0, 0): staging[0][:], (0, 1): staging[1][:], (1, 0): next_stage, (1, 1): staging[3][:]}

        def cast_wg(b, a, pair, copy):
            src = wg_raw[(b, a)][:].rearrange("p j (m t) -> p m j t", t=PACK)
            dst = wg_stage[(b, a)].rearrange("p (t m j) -> p m j t", t=PACK, j=PACK)
            copy(out=dst[:, :, :, 2 * pair : 2 * pair + 2], in_=src[:, :, :, 2 * pair : 2 * pair + 2])

        def quantise_wg(b, a, lo, hi):
            nc.vector.quantize_mx(
                out=wg_codes[(b, a)][:, lo:hi].bitcast(FP8X4),
                scales=wg_plane[(b, a)][:, lo:hi],
                in_=wg_stage[(b, a)][:, PACK * lo : PACK * hi],
            )

        h_codes = {(c, b): held([P, CHUNK], U32, "h_codes%d%d" % (c, b)) for c in range(CHUNKS) for b in range(2)}
        h_plane = {(c, b): held([P, CHUNK], U8, "h_plane%d%d" % (c, b)) for c in range(CHUNKS) for b in range(2)}

        def gate_pass(c, b, t, a, bank):
            nc.tensor.matmul_mx(
                out=bank[:],
                lhsT=wg_codes[(b, a)][:, P * t : P * (t + 1)].bitcast(FP8X4),
                lhsT_scale=wg_plane[(b, a)][:, P * t : P * (t + 1)],
                rhs=words[(c, a)][:].bitcast(FP8X4),
                rhs_scale=planes[c][4 * a :, :],
                start=(a == 0),
                stop=(a == 1),
            )

        def gate_part(c, b, first_bank, by_pass=False):
            act = ring.tile([P, PACK, CHUNK], F32, name="act")
            if by_pass:
                for t in range(PACK):
                    gate_pass(c, b, t, 0, banks[first_bank + t])
            for t in range(PACK):
                for a in range(1 if by_pass else 0, 2):
                    gate_pass(c, b, t, a, banks[first_bank + t])
                nc.scalar.activation(out=act[:, t, :], in_=banks[first_bank + t][:], func=SILU)
            return act

        def up_pass(c, b, t, a, cols, acc):
            nc.tensor.matmul_mx(
                out=acc,
                lhsT=wu[(b, a)][:, t, :].bitcast(FP8X4),
                lhsT_scale=wu_plane[4 * a :, t, b, :],
                rhs=words[(c, a)][:, cols].bitcast(FP8X4),
                rhs_scale=planes[c][4 * a :, cols],
                start=(a == 0),
                stop=(a == 1),
            )

        def up_view(bank):
            return bank[:].rearrange("p (t n) -> p t n", t=PACK)

        def quarter(q):
            return slice(QUARTER * q, QUARTER * (q + 1))

        def up_sums(c, b, q, bank):
            for t in range(PACK):
                for a in range(2):
                    up_pass(c, b, t, a, quarter(q), up_view(bank)[:, t, :])

        def multiply(q, act, up, stage, engine=nc.vector, count=1):
            engine.tensor_tensor(
                out=stage[:, PASS * q : PASS * (q + count)].rearrange("p (n i t) -> p n t i", i=2, t=PACK),
                in0=up.rearrange("p t (n i) -> p n t i", i=2),
                in1=act[:, :, QUARTER * q : QUARTER * (q + count)].rearrange("p t (n i) -> p n t i", i=2),
                op=MULT,
            )

        def share_first_quarter(act, stage):
            parked = ring.tile([P, CHUNK], F32, name="parked")
            nc.scalar.copy(out=parked[:], in_=banks[UP][:])
            multiply(0, act, up_view(parked), stage, nc.gpsimd)

        def quantise_h(c, b, stage, lo=0, hi=CHUNK):
            nc.vector.quantize_mx(
                out=h_codes[(c, b)][:, lo:hi].bitcast(FP8X4),
                scales=h_plane[(c, b)][:, lo:hi],
                in_=stage[:, PACK * lo : PACK * hi],
            )

        def down_pass(c, b, nt, cols, acc):
            nc.tensor.matmul_mx(
                out=acc,
                lhsT=wd[:, b, P * nt : P * (nt + 1)].bitcast(FP8X4),
                lhsT_scale=wd_plane[:].bitcast(U8)[4 * b :, P * nt : P * (nt + 1)],
                rhs=h_codes[(c, b)][:, cols].bitcast(FP8X4),
                rhs_scale=h_plane[(c, b)][:, cols],
                start=(b == 0),
                stop=(b == 1),
            )

        def down(c, nt, cols, acc):
            for b in range(2):
                down_pass(c, b, nt, cols, acc)

        def down_chunk(c, next_stage):
            sums = []
            for nt in range(2):
                down(c, nt, slice(0, CHUNK), banks[nt][:])
                if nt == 0:
                    y = ring.tile([P, CHUNK], F32, name="y")
                else:
                    y = next_stage[:].bitcast(F32)[:, :CHUNK]
                nc.scalar.copy(out=y[:], in_=banks[nt][:])
                sums.append(y)
            return sums

        def gate_and_store(c, nt, y):
            res = ring.tile([P, CHUNK], F32, name="res")
            nc.vector.tensor_tensor(out=res[:], in0=gate[nt][:].indirect(chunk_list(c)), in1=y[:], op=MULT)
            nc.sync.dma_start(out=out[P * nt : P * (nt + 1), CHUNK * c : CHUNK * (c + 1)], in_=res[:])

        last_gates = wg_raw[(1, 1)][:, 0:2, :]

        def pick_last_gates(nt):
            nc.vector.tensor_copy(out=last_gates[:, nt, :], in_=gate[nt][:].indirect(chunk_list(LAST)))

        def quarter_view(q):
            return banks[q][:, : 2 * QUARTER].rearrange("p (nt n) -> p nt n", nt=2)

        def finish_last_quarter(q):
            cols = slice(QUARTER * q, QUARTER * (q + 1))
            for nt in range(2):
                down(LAST, nt, cols, quarter_view(q)[:, nt, :])
            res = held([P, 2, QUARTER], F32, "res_last%d" % q)
            nc.vector.tensor_tensor(out=res[:], in0=quarter_view(q), in1=last_gates[:, :, cols], op=MULT)
            c0 = CHUNK * LAST + QUARTER * q
            nc.sync.dma_start(out=out[:, c0 : c0 + QUARTER].rearrange("(nt p) j -> p nt j", p=P), in_=res[:])

        def finish_at_the_end():
            cols = slice(CHUNK - QUARTER, CHUNK)
            sums = [banks[PACK - 1 + nt][:, :QUARTER] for nt in range(2)]
            for b in range(2):
                for nt in range(2):
                    down_pass(LAST, b, nt, cols, sums[nt])
            for nt, queue in enumerate((nc.scalar, nc.sync)):
                res = held([P, QUARTER], F32, "res_end%d" % nt)
                nc.vector.tensor_tensor(out=res[:], in0=sums[nt], in1=last_gates[:, nt, cols], op=MULT)
                queue.dma_start(out=out[P * nt : P * (nt + 1), J - QUARTER :], in_=res[:])

        everything = slice(0, CHUNK)
        gather_words(0, 0)
        permute_wu_first(0)
        gather_words(1, 0)
        gather_words(2, 0)
        gather_words(LAST, 0)
        for c in range(2):
            for t in range(PACK):
                up_pass(c, 0, t, 0, everything, banks[PACK * c + t][:])

        permute_wu_first(1)
        kept_up = [held([P, PACK, CHUNK], F32, "kept_up%d" % c) for c in range(2)]
        for c in range(2):
            gather_words(c, 1)
            for t in range(PACK):
                up_pass(c, 0, t, 1, everything, banks[PACK * c + t][:])
                nc.scalar.copy(out=kept_up[c][:, t, :], in_=banks[PACK * c + t][:])
        gather_words(2, 1)
        for q in range(PACK):
            up_sums(2, 0, q, banks[q])
        for pair in range(2):
            cast_wg(0, 0, pair, nc.vector.tensor_copy)
        quantise_wg(0, 0, 0, PASS)
        cast_wg(0, 1, 0, nc.vector.tensor_copy)
        cast_wg(0, 1, 1, nc.scalar.copy)
        for pair in range(2):
            quantise_wg(0, 1, PASS // 2 * pair, PASS // 2 * (pair + 1))
        act_2 = gate_part(2, 0, UP, by_pass=True)
        permute_wu_second()
        gather_words(LAST, 1, tag="staging1")
        gate.append(keep.tile([P, T], F32, name="gate1", tag="tab0", align_bytes=64))
        nc.sync.dma_start(out=gate[1][:], in_=gT[P:, :])
        act_0 = gate_part(0, 0, UP)
        for q in range(PACK):
            multiply(q, act_2, up_view(banks[q]), staging[2])
        act_1 = gate_part(1, 0, 0)
        for pair in range(2):
            cast_wg(1, 0, pair, nc.vector.tensor_copy)
        quantise_h(2, 0, staging[2])
        quantise_wg(1, 0, 0, PASS)
        for pair in range(2):
            cast_wg(1, 1, pair, nc.scalar.copy)
        multiply(0, act_0, kept_up[0][:], h_stage, count=4)
        for q in range(PACK):
            up_sums(0, 1, q, banks[UP + q])
        for pair in range(2):
            quantise_wg(1, 1, PASS // 2 * pair, PASS // 2 * (pair + 1))
        multiply(2, act_1, kept_up[1][:, :, 2 * QUARTER :], next_stage, count=2)
        quantise_h(0, 0, h_stage)
        act = gate_part(0, 1, 0, by_pass=True)
        pick_last_gates(0)
        for q in range(2):
            multiply(q, act_1, kept_up[1][:, :, quarter(q)], next_stage, nc.gpsimd)
        for q in range(PACK):
            multiply(q, act, up_view(banks[UP + q]), staging[0])
        quantise_h(0, 1, staging[0])
        quantise_h(1, 0, next_stage)

        stages = (next_stage, staging[2], staging[0], staging[2])
        for done, (c, b) in enumerate(((1, 1), (2, 1), (LAST, 0))):
            act = gate_part(c, b, 0)
            stage = stages[done]
            for q in range(PACK):
                up_sums(c, b, q, banks[UP + q])
                if q == 0:
                    share_first_quarter(act, stage)
                else:
                    multiply(q, act, up_view(banks[UP + q]), stage)
                if q == PACK - 2:
                    sums = down_chunk(done, stages[done + 1])
            gate_and_store(done, 0, sums[0])
            quantise_h(c, b, stage)
            gate_and_store(done, 1, sums[1])
            if done == 1:
                pick_last_gates(1)

        act = gate_part(LAST, 1, 0)
        for q in range(PACK + 1):
            if q < PACK:
                up_sums(LAST, 1, q, banks[UP + q])
                multiply(q, act, up_view(banks[UP + q]), stages[3])
            if q >= 1:
                quantise_h(LAST, 1, stages[3], QUARTER * (q - 1), QUARTER * q)
        for q in range(PACK - 1):
            finish_last_quarter(q)
        finish_at_the_end()
